import numpy as np
import ml_dtypes


def mxq(x, axis, fmt="e4m3"):
    dtype, down = {"e4m3": (ml_dtypes.float8_e4m3fn, 7), "e5m2": (ml_dtypes.float8_e5m2, 14)}[fmt]
    v = np.moveaxis(np.asarray(x, np.float32).astype(ml_dtypes.bfloat16).astype(np.float64), axis, -1)
    blocks = v.reshape(v.shape[:-1] + (-1, 32))
    amax = np.abs(blocks).max(-1, keepdims=True)
    byte = np.maximum(np.where(amax > 0, np.frexp(amax)[1] - 1 + 127, 0) - down, 1)
    scale = np.exp2(byte - 127.0)
    codes = (blocks / scale).astype(np.float32).astype(dtype).astype(np.float64)
    return np.moveaxis((codes * scale).reshape(v.shape), -1, axis)


WIDE = False


def mx_kscale(k):
    if not WIDE:
        return np.ones(k)
    levels = np.array([24, -24, 12, -12, 0])
    if k % 512:
        return np.exp2(np.random.permutation(np.resize(levels, k // 32))).repeat(32)
    a = np.empty((k // 512, 16))
    for p in range(k // 512):
        a[p, :8] = np.random.permutation(np.resize(levels, 8))
        for g in range(8):
            far = levels[np.abs(levels - a[p, g]) >= 10]
            a[p, g + 8] = far[np.random.randint(len(far))]
    return np.exp2(a.ravel()).repeat(32)


def f64(x):
    return np.asarray(x).astype(np.float64)


def striped(idx):
    return np.tile(idx.reshape(-1, 16).T, (8, 1)).astype(np.uint16)


def unstriped(offs):
    return offs[:16].T.reshape(-1).astype(np.int64)


def striped8(idx):
    return np.concatenate([v.reshape(-1, 16).T for v in idx]).astype(np.uint16)


def unstriped8(offs):
    return np.stack([offs[16 * g:16 * g + 16].T.reshape(-1) for g in range(8)]).astype(np.int64)


E2M1 = np.array([0.0, 0.5, 1.0, 1.5, 2.0, 3.0, 4.0, 6.0, -0.0, -0.5, -1.0, -1.5, -2.0, -3.0, -4.0, -6.0])


def pack_weight(w, fmt):
    k, n = w.shape
    w = f64(np.asarray(w, np.float32).astype(ml_dtypes.bfloat16)).reshape(k // 32, 32, n)
    amax = np.abs(w).max(1)
    if fmt == "e4m3":
        byte = np.frexp(amax)[1] - 1 + 127 - 7
    else:
        mant, ex = np.frexp(amax / 6.0)
        byte = np.where(mant > 0.5, ex, ex - 1) + 127
    byte = np.clip(np.where(amax > 0, byte, 1), 1, 254)
    scaled = (w * np.exp2(127.0 - byte)[:, None, :]).reshape(k, n).astype(np.float32)
    by_word = np.ascontiguousarray(scaled.reshape(k // 512, 128, 4, n).transpose(0, 1, 3, 2))
    if fmt == "e4m3":
        words = by_word.astype(ml_dtypes.float8_e4m3fn).view(np.uint8)
    else:
        c = by_word.astype(ml_dtypes.float4_e2m1fn).view(np.uint8) & 0xF
        words = (c[..., 0::2] | (c[..., 1::2] << 4)).reshape(k // 512, 128, 2 * n)
    return np.ascontiguousarray(words), np.ascontiguousarray(byte.astype(np.uint8).reshape(k // 512, 16, n))


def unpack_weight(words, scales, fmt):
    g, _, n = scales.shape
    words = np.ascontiguousarray(words).reshape(g, 128, n, -1)
    if fmt == "e4m3":
        vals = words.view(ml_dtypes.float8_e4m3fn).astype(np.float64)
    else:
        nib = np.empty((g, 128, n, 4), np.uint8)
        nib[..., 0::2] = words & 0xF
        nib[..., 1::2] = words >> 4
        vals = E2M1[nib]
    vals = vals * np.repeat(np.exp2(scales.astype(np.float64) - 127.0), 8, axis=1)[..., None]
    return vals.transpose(0, 1, 3, 2).reshape(g * 512, n)


def sigm(f):
    return 1.0 / (1.0 + np.exp(-np.maximum(f, -700.0)))


K, L, R, N, T, J = 512, 512, 512, 512, 2048, 1024


def setup_inputs():
    n = np.random.standard_normal
    s = mx_kscale(K)[:, None]
    s2 = mx_kscale(L)[:, None]
    u = mx_kscale(R)[:, None]
    p_tab = pack_weight(n((L, T)) * s2, "e4m3")
    p_wa = pack_weight(n((K, R)) / np.sqrt(K) / s * u.T, "e2m1")
    return {
        "tab_words": p_tab[0],
        "tab_scales": p_tab[1],
        "xT": (n((K, T)) * s).astype(np.float32),
        "wgt2": np.repeat(np.random.uniform(0.5, 2.0, (8, J)), 16, axis=0).astype(np.float32),
        "wa_words": p_wa[0],
        "wa_scales": p_wa[1],
        "wb": (n((L, R)) / np.sqrt(L) / s2).astype(np.float32),
        "wd": (n((R, N)) / np.sqrt(R) / u).astype(np.float32),
        "offs": striped(np.random.permutation(T)[:J]),
        "offs2": striped8(np.stack([np.random.permutation(T)[:J] for _ in range(8)])),
    }


def reference(tab_words, tab_scales, xT, wgt2, wa_words, wa_scales, wb, wd, offs, offs2):
    idx = unstriped(offs)
    idx2 = unstriped8(offs2)
    tab_ = unpack_weight(tab_words, tab_scales, "e4m3")[:, idx]
    rows = np.arange(K)
    xg = f64(wgt2)[rows // 4 % 128] * f64(xT)[rows[:, None], idx2[rows % 512 // 64]]
    xT_ = mxq(xg, 0, "e4m3")
    wa_ = unpack_weight(wa_words, wa_scales, "e2m1")
    wb_ = mxq(f64(wb), 0, "e4m3")
    ya = wa_.T @ xT_
    yb = wb_.T @ tab_
    h = ya * sigm(yb)
    h_ = mxq(h, 0, "e4m3")
    wd_ = mxq(f64(wd), 0, "e4m3")
    y = wd_.T @ h_
    return y

@@ -1,0 +1,221 @@
+from contextlib import ExitStack
+
+import concourse.mybir as mybir
+
+K, L, R, N, T, J = 512, 512, 512, 512, 2048, 1024
+FLOPS = 2 * J * (K * R + L * R + R * N)
+
+F32 = mybir.dt.float32
+BF16 = mybir.dt.bfloat16
+I32 = mybir.dt.int32
+U32 = mybir.dt.uint32
+U16 = mybir.dt.uint16
+U8 = mybir.dt.uint8
+FP8X4 = mybir.dt.float8_e4m3fn_x4
+FP4X4 = mybir.dt.float4_e2m1fn_x4
+MULT = mybir.AluOpType.mult
+SIGMOID = mybir.ActivationFunctionType.Sigmoid
+
+P = 128
+PACK = 4
+GROUP = 16
+NB = 128
+CH = 256
+
+
+def tile_list_htabg_gate_none_kernel(
+    tc, tab_words, tab_scales, xT, wgt2, wa_words, wa_scales, wb, wd, offs, offs2, out
+):
+    nc = tc.nc
+    with ExitStack() as ctx:
+        keep = ctx.enter_context(tc.tile_pool(name="keep", bufs=1))
+        ystage = ctx.enter_context(tc.tile_pool(name="ystage", bufs=8))
+        ps1 = ctx.enter_context(tc.psum_pool(name="ps1", bufs=4))
+        ps2 = ctx.enter_context(tc.psum_pool(name="ps2", bufs=4))
+
+        def sb(name, shape, dtype):
+            return keep.tile(shape, dtype, name=name, align_bytes=64)
+
+        tab_list = keep.tile([P, J // GROUP], U16, name="tab_list")
+        head_lists = keep.tile([P, J // GROUP], U16, name="head_lists")
+        tab_w = sb("tab_w", [P, T], I32)
+        tab_s = sb("tab_s", [P, T // 4], I32)
+        wa_w_raw = sb("wa_w_raw", [P, R // 2], I32)
+        wa_s_raw = sb("wa_s_raw", [P, R // 4], I32)
+        wb_raw = sb("wb_raw", [P, PACK, R], F32)
+        wd_raw = sb("wd_raw", [P, PACK, N], F32)
+        wgt = sb("wgt", [P, J], F32)
+        planes = [sb("plane%d" % i, [P, T], F32) for i in range(PACK)]
+
+        warm = sb("warm", [P, 8], F32)
+        nc.vector.memset(tab_s[:], 0)
+        nc.vector.memset(wa_s_raw[:], 0)
+        nc.vector.memset(warm[:, 0:1], 0.0)
+
+        x_planes = xT.rearrange("(p i) t -> i p t", i=PACK)
+
+        def load_scales(queue, dst, src):
+            for q in range(4):
+                queue.dma_start(out=dst[32 * q : 32 * q + 4, :], in_=src[0, 4 * q : 4 * q + 4, :].bitcast(I32))
+
+        nc.sync.dma_start(tab_list[:], offs)
+        nc.sync.dma_start(out=tab_w[:], in_=tab_words[0].rearrange("p t i -> p (t i)").bitcast(I32))
+        load_scales(nc.scalar, tab_s, tab_scales)
+        nc.scalar.activation(warm[:, 1:2], warm[:, 0:1], SIGMOID)
+        nc.sync.dma_start(out=wb_raw[:], in_=wb.rearrange("(p i) r -> p i r", i=PACK))
+        nc.sync.dma_start(out=wgt[:], in_=wgt2)
+        nc.sync.dma_start(head_lists[:], offs2)
+        nc.sync.dma_start(out=planes[0][:], in_=x_planes[0])
+        nc.sync.dma_start(out=wa_w_raw[:], in_=wa_words[0].bitcast(I32))
+        load_scales(nc.sync, wa_s_raw, wa_scales)
+        nc.sync.dma_start(out=planes[1][:], in_=x_planes[1])
+        nc.sync.dma_start(out=wd_raw[:], in_=wd.rearrange("(p i) n -> p i n", i=PACK))
+        nc.sync.dma_start(out=planes[2][:], in_=x_planes[2])
+        nc.sync.dma_start(out=planes[3][:], in_=x_planes[3])
+
+        v_codes = sb("v_codes", [P, J], U32)
+        v_scales = sb("v_scales", [P, J], U8)
+        nc.vector.tensor_copy(v_scales[:], tab_s[:].bitcast(U8).indirect(tab_list[:]))
+        nc.vector.tensor_copy(v_codes[:], tab_w[:].bitcast(U32).indirect(tab_list[:]))
+
+        wb_bf = sb("wb_bf", [P, R * PACK], BF16)
+        wb_codes = sb("wb_codes", [P, R], U32)
+        wb_scales = sb("wb_scales", [P, R], U8)
+        nc.scalar.copy(
+            out=wb_bf[:].rearrange("p (t m i) -> p m t i", t=PACK, i=PACK),
+            in_=wb_raw[:].rearrange("p i (m t) -> p m t i", t=PACK),
+        )
+        nc.vector.quantize_mx(out=wb_codes[:].bitcast(FP8X4), scales=wb_scales[:], in_=wb_bf[:])
+
+        gate = sb("gate", [P, J, PACK], F32)
+        for b in range(J // NB):
+            cols = slice(b * NB, (b + 1) * NB)
+            acc = ps1.tile([P, PACK, NB], F32, name="acc")
+            for t in range(PACK):
+                m = slice(t * P, (t + 1) * P)
+                nc.tensor.matmul_mx(
+                    out=acc[:, t, :],
+                    lhsT=wb_codes[:, m].bitcast(FP8X4), lhsT_scale=wb_scales[:, m],
+                    rhs=v_codes[:, cols].bitcast(FP8X4), rhs_scale=v_scales[:, cols],
+                    start=True, stop=True,
+                )
+            nc.scalar.activation(gate[:, cols, :], acc[:].rearrange("p t n -> p n t"), SIGMOID)
+
+        picked = sb("picked", [P, PACK, J], F32)
+
+        def gather(i, lo, hi):
+            nc.vector.tensor_tensor(
+                picked[:, i, lo:hi],
+                planes[i][:].indirect(head_lists[:, lo // GROUP : hi // GROUP]),
+                wgt[:, lo:hi],
+                MULT,
+            )
+
+        x_bf = sb("x_bf", [P, J, PACK], BF16)
+
+        def lay_pair(i, lo, hi):
+            nc.scalar.copy(out=x_bf[:, lo:hi, i : i + 2], in_=picked[:, i : i + 2, lo:hi].rearrange("p i j -> p j i"))
+
+        gather(0, 0, J // 2)
+        gather(0, J // 2, J)
+
+        wa_codes = sb("wa_codes", [P, 2 * R], U8)
+        wa_sc = sb("wa_sc", [P, R], U8)
+        nc.vector.tensor_copy(
+            out=wa_codes[:].bitcast(U16).rearrange("p (t m) -> p t m", t=PACK),
+            in_=wa_w_raw[:].bitcast(U16).rearrange("p (m t) -> p t m", t=PACK),
+        )
+        nc.vector.tensor_copy(
+            out=wa_sc[:].rearrange("p (t m) -> p t m", t=PACK),
+            in_=wa_s_raw[:].bitcast(U8).rearrange("p (m t) -> p t m", t=PACK),
+        )
+
+        gather(1, 0, J // 2)
+        gather(1, J // 2, J)
+        lay_pair(0, 0, J // 2)
+        lay_pair(0, J // 2, J)
+
+        wd_bf = sb("wd_bf", [P, N * PACK], BF16)
+        wd_codes = sb("wd_codes", [P, N], U32)
+        wd_scales = sb("wd_scales", [P, N], U8)
+        nc.vector.tensor_copy(
+            out=wd_bf[:].rearrange("p (c e i) -> p c i e", e=4, i=PACK),
+            in_=wd_raw[:].rearrange("p i (c e) -> p c i e", e=4),
+        )
+        gather(2, 0, J // 2)
+        nc.vector.quantize_mx(out=wd_codes[:].bitcast(FP8X4), scales=wd_scales[:], in_=wd_bf[:])
+        gather(2, J // 2, J)
+
+        x_codes = sb("x_codes", [P, J], U32)
+        x_scales = sb("x_scales", [P, J], U8)
+        h_bf = sb("h_bf", [P, J, PACK], BF16)
+        h_codes = sb("h_codes", [P, J], U32)
+        h_scales = sb("h_scales", [P, J], U8)
+        out_v = out.rearrange("(a p) j -> p a j", p=P)
+
+        def quant(codes, scales, src, lo, hi):
+            nc.vector.quantize_mx(
+                out=codes[:, lo:hi].bitcast(FP8X4), scales=scales[:, lo:hi],
+                in_=src[:, lo:hi, :].rearrange("p j i -> p (j i)"),
+            )
+
+        def last_plane(c):
+            gather(3, c * CH, (c + 1) * CH)
+            lay_pair(2, c * CH, (c + 1) * CH)
+
+        def quant_x(c):
+            quant(x_codes, x_scales, x_bf, c * CH, (c + 1) * CH)
+
+        def gated(b):
+            cols = slice(b * NB, (b + 1) * NB)
+            acc = ps1.tile([P, PACK, NB], F32, name="acc")
+            for t in range(PACK):
+                nc.tensor.matmul_mx(
+                    out=acc[:, t, :],
+                    lhsT=wa_codes[:, 2 * t * P : 2 * (t + 1) * P].bitcast(FP4X4),
+                    lhsT_scale=wa_sc[:, t * P : (t + 1) * P],
+                    rhs=x_codes[:, cols].bitcast(FP8X4), rhs_scale=x_scales[:, cols],
+                    start=True, stop=True,
+                )
+            nc.vector.tensor_tensor(h_bf[:, cols, :], acc[:].rearrange("p t n -> p n t"), gate[:, cols, :], MULT)
+
+        def second(c):
+            lo, hi = c * CH, (c + 1) * CH
+            quant(h_codes, h_scales, h_bf, lo, hi)
+            for u in range(2):
+                yacc = ps2.tile([P, 2, CH], F32, name="yacc")
+                for a in range(2):
+                    m = slice((2 * u + a) * P, (2 * u + a + 1) * P)
+                    nc.tensor.matmul_mx(
+                        out=yacc[:, a, :],
+                        lhsT=wd_codes[:, m].bitcast(FP8X4), lhsT_scale=wd_scales[:, m],
+                        rhs=h_codes[:, lo:hi].bitcast(FP8X4), rhs_scale=h_scales[:, lo:hi],
+                        start=True, stop=True,
+                    )
+                ysb = ystage.tile([P, 2, CH], F32, name="ysb")
+                if c == J // CH - 1 and u == 1:
+                    nc.vector.tensor_copy(out=ysb[:], in_=yacc[:])
+                else:
+                    nc.scalar.copy(out=ysb[:], in_=yacc[:])
+                nc.sync.dma_start(out=out_v[:, 2 * u : 2 * u + 2, lo:hi], in_=ysb[:])
+
+        last_plane(0)
+        last_plane(1)
+        last_plane(2)
+        quant_x(0)
+        last_plane(3)
+        quant_x(1)
+        gated(0)
+        gated(1)
+        quant_x(2)
+        gated(2)
+        second(0)
+        gated(3)
+        quant_x(3)
+        gated(4)
+        second(1)
+        gated(5)
+        gated(6)
+        second(2)
+        gated(7)
+        second(3)

@@ -1,3 +1,4 @@
+import math
 from contextlib import ExitStack
 
 import concourse.mybir as mybir
@@ -29,28 +30,35 @@ def tile_list_htabg_gate_none_kernel(
     nc = tc.nc
     with ExitStack() as ctx:
         keep = ctx.enter_context(tc.tile_pool(name="keep", bufs=1))
-        ystage = ctx.enter_context(tc.tile_pool(name="ystage", bufs=8))
+        late = ctx.enter_context(tc.tile_pool(name="late", bufs=1))
+        ystage = ctx.enter_context(tc.tile_pool(name="ystage", bufs=10))
         ps1 = ctx.enter_context(tc.psum_pool(name="ps1", bufs=4))
         ps2 = ctx.enter_context(tc.psum_pool(name="ps2", bufs=4))
 
-        def sb(name, shape, dtype):
-            return keep.tile(shape, dtype, name=name, align_bytes=64)
+        def sb(name, shape, dtype, tag=None):
+            return keep.tile(shape, dtype, name=name, tag=tag or name, align_bytes=64)
 
         tab_list = keep.tile([P, J // GROUP], U16, name="tab_list")
         head_lists = keep.tile([P, J // GROUP], U16, name="head_lists")
         tab_w = sb("tab_w", [P, T], I32)
-        tab_s = sb("tab_s", [P, T // 4], I32)
         wa_w_raw = sb("wa_w_raw", [P, R // 2], I32)
-        wa_s_raw = sb("wa_s_raw", [P, R // 4], I32)
-        wb_raw = sb("wb_raw", [P, PACK, R], F32)
-        wd_raw = sb("wd_raw", [P, PACK, N], F32)
-        wgt = sb("wgt", [P, J], F32)
-        planes = [sb("plane%d" % i, [P, T], F32) for i in range(PACK)]
-
-        warm = sb("warm", [P, 8], F32)
+        tab_s = sb("tab_s", [P, T // 4], I32)
+        late_shapes = [("wb_raw", [P, PACK, R], F32), ("wa_s_raw", [P, R // 4], I32),
+                       ("wgt", [P, J], F32), ("wd_raw", [P, PACK, N], F32)]
+        late_shapes += [("plane%d" % i, [P, T], F32) for i in range(PACK)]
+        late_at = {}
+        words = 0
+        for name, shape, dtype in late_shapes:
+            late_at[name] = 4 * words
+            words += math.prod(shape[1:])
+        warm = late.tile([P, words], F32, name="warm", align_bytes=64, offset=0)
         nc.vector.memset(tab_s[:], 0)
-        nc.vector.memset(wa_s_raw[:], 0)
         nc.vector.memset(warm[:, 0:1], 0.0)
+        nc.scalar.activation(warm[:, 1:2], warm[:, 0:1], SIGMOID)
+        lt = {name: late.tile(shape, dtype, name=name, align_bytes=64, offset=late_at[name]) for name, shape, dtype in late_shapes}
+        wb_raw, wa_s_raw, wgt, wd_raw = lt["wb_raw"], lt["wa_s_raw"], lt["wgt"], lt["wd_raw"]
+        planes = [lt["plane%d" % i] for i in range(PACK)]
+        nc.vector.memset(wa_s_raw[:], 0)
 
         x_planes = xT.rearrange("(p i) t -> i p t", i=PACK)
 
@@ -59,24 +67,28 @@ def tile_list_htabg_gate_none_kernel(
                 queue.dma_start(out=dst[32 * q : 32 * q + 4, :], in_=src[0, 4 * q : 4 * q + 4, :].bitcast(I32))
 
         nc.sync.dma_start(tab_list[:], offs)
-        nc.sync.dma_start(out=tab_w[:], in_=tab_words[0].rearrange("p t i -> p (t i)").bitcast(I32))
-        load_scales(nc.scalar, tab_s, tab_scales)
-        nc.scalar.activation(warm[:, 1:2], warm[:, 0:1], SIGMOID)
-        nc.sync.dma_start(out=wb_raw[:], in_=wb.rearrange("(p i) r -> p i r", i=PACK))
-        nc.sync.dma_start(out=wgt[:], in_=wgt2)
         nc.sync.dma_start(head_lists[:], offs2)
-        nc.sync.dma_start(out=planes[0][:], in_=x_planes[0])
         nc.sync.dma_start(out=wa_w_raw[:], in_=wa_words[0].bitcast(I32))
+        nc.sync.dma_start(out=tab_w[:], in_=tab_words[0].rearrange("p t i -> p (t i)").bitcast(I32))
+        load_scales(nc.sync, tab_s, tab_scales)
+        nc.sync.dma_start(out=wb_raw[:], in_=wb.rearrange("(p i) r -> p i r", i=PACK))
         load_scales(nc.sync, wa_s_raw, wa_scales)
-        nc.sync.dma_start(out=planes[1][:], in_=x_planes[1])
+        nc.sync.dma_start(out=wgt[:], in_=wgt2)
+        for i in range(PACK):
+            nc.sync.dma_start(out=planes[i][:], in_=x_planes[i])
         nc.sync.dma_start(out=wd_raw[:], in_=wd.rearrange("(p i) n -> p i n", i=PACK))
-        nc.sync.dma_start(out=planes[2][:], in_=x_planes[2])
-        nc.sync.dma_start(out=planes[3][:], in_=x_planes[3])
+
+        wa_codes = sb("wa_codes", [P, 2 * R], U8)
+        wa_sc = sb("wa_sc", [P, R], U8)
+        nc.vector.tensor_copy(
+            out=wa_codes[:].bitcast(U16).rearrange("p (t m) -> p t m", t=PACK),
+            in_=wa_w_raw[:].bitcast(U16).rearrange("p (m t) -> p t m", t=PACK),
+        )
 
         v_codes = sb("v_codes", [P, J], U32)
         v_scales = sb("v_scales", [P, J], U8)
-        nc.vector.tensor_copy(v_scales[:], tab_s[:].bitcast(U8).indirect(tab_list[:]))
         nc.vector.tensor_copy(v_codes[:], tab_w[:].bitcast(U32).indirect(tab_list[:]))
+        nc.vector.tensor_copy(v_scales[:], tab_s[:].bitcast(U8).indirect(tab_list[:]))
 
         wb_bf = sb("wb_bf", [P, R * PACK], BF16)
         wb_codes = sb("wb_codes", [P, R], U32)
@@ -85,7 +97,12 @@ def tile_list_htabg_gate_none_kernel(
             out=wb_bf[:].rearrange("p (t m i) -> p m t i", t=PACK, i=PACK),
             in_=wb_raw[:].rearrange("p i (m t) -> p m t i", t=PACK),
         )
+
         nc.vector.quantize_mx(out=wb_codes[:].bitcast(FP8X4), scales=wb_scales[:], in_=wb_bf[:])
+        nc.vector.tensor_copy(
+            out=wa_sc[:].rearrange("p (t m) -> p t m", t=PACK),
+            in_=wa_s_raw[:].bitcast(U8).rearrange("p (m t) -> p t m", t=PACK),
+        )
 
         gate = sb("gate", [P, J, PACK], F32)
         for b in range(J // NB):
@@ -101,50 +118,41 @@ def tile_list_htabg_gate_none_kernel(
                 )
             nc.scalar.activation(gate[:, cols, :], acc[:].rearrange("p t n -> p n t"), SIGMOID)
 
-        picked = sb("picked", [P, PACK, J], F32)
+        half = J // 2
+        picked = {
+            (0, 0): sb("picked00", [P, 2, half], F32, tag="wb_bf"),
+            (0, 1): sb("picked01", [P, 2, half], F32),
+            (1, 0): sb("picked10", [P, 2, half], F32),
+            (1, 1): sb("picked11", [P, 2, half], F32),
+        }
 
         def gather(i, lo, hi):
+            base = lo // half * half
             nc.vector.tensor_tensor(
-                picked[:, i, lo:hi],
+                picked[i // 2, lo // half][:, i % 2, lo - base : hi - base],
                 planes[i][:].indirect(head_lists[:, lo // GROUP : hi // GROUP]),
                 wgt[:, lo:hi],
                 MULT,
             )
 
-        x_bf = sb("x_bf", [P, J, PACK], BF16)
-
         def lay_pair(i, lo, hi):
-            nc.scalar.copy(out=x_bf[:, lo:hi, i : i + 2], in_=picked[:, i : i + 2, lo:hi].rearrange("p i j -> p j i"))
+            base = lo // half * half
+            nc.scalar.copy(
+                out=x_bf[:, lo:hi, i : i + 2],
+                in_=picked[i // 2, lo // half][:, :, lo - base : hi - base].rearrange("p i j -> p j i"),
+            )
 
-        gather(0, 0, J // 2)
-        gather(0, J // 2, J)
-
-        wa_codes = sb("wa_codes", [P, 2 * R], U8)
-        wa_sc = sb("wa_sc", [P, R], U8)
-        nc.vector.tensor_copy(
-            out=wa_codes[:].bitcast(U16).rearrange("p (t m) -> p t m", t=PACK),
-            in_=wa_w_raw[:].bitcast(U16).rearrange("p (m t) -> p t m", t=PACK),
-        )
-        nc.vector.tensor_copy(
-            out=wa_sc[:].rearrange("p (t m) -> p t m", t=PACK),
-            in_=wa_s_raw[:].bitcast(U8).rearrange("p (m t) -> p t m", t=PACK),
-        )
-
-        gather(1, 0, J // 2)
-        gather(1, J // 2, J)
+        for i in range(2):
+            gather(i, 0, J // 2)
+            gather(i, J // 2, J)
+        x_bf = sb("x_bf", [P, J, PACK], BF16, tag="wb_codes")
         lay_pair(0, 0, J // 2)
         lay_pair(0, J // 2, J)
+        gather(2, 0, J // 2)
+        gather(2, J // 2, J)
 
-        wd_bf = sb("wd_bf", [P, N * PACK], BF16)
         wd_codes = sb("wd_codes", [P, N], U32)
         wd_scales = sb("wd_scales", [P, N], U8)
-        nc.vector.tensor_copy(
-            out=wd_bf[:].rearrange("p (c e i) -> p c i e", e=4, i=PACK),
-            in_=wd_raw[:].rearrange("p i (c e) -> p c i e", e=4),
-        )
-        gather(2, 0, J // 2)
-        nc.vector.quantize_mx(out=wd_codes[:].bitcast(FP8X4), scales=wd_scales[:], in_=wd_bf[:])
-        gather(2, J // 2, J)
 
         x_codes = sb("x_codes", [P, J], U32)
         x_scales = sb("x_scales", [P, J], U8)
@@ -179,11 +187,10 @@ def tile_list_htabg_gate_none_kernel(
                 )
             nc.vector.tensor_tensor(h_bf[:, cols, :], acc[:].rearrange("p t n -> p n t"), gate[:, cols, :], MULT)
 
-        def second(c):
-            lo, hi = c * CH, (c + 1) * CH
+        def second(lo, hi):
             quant(h_codes, h_scales, h_bf, lo, hi)
             for u in range(2):
-                yacc = ps2.tile([P, 2, CH], F32, name="yacc")
+                yacc = ps2.tile([P, 2, hi - lo], F32, name="yacc")
                 for a in range(2):
                     m = slice((2 * u + a) * P, (2 * u + a + 1) * P)
                     nc.tensor.matmul_mx(
@@ -192,8 +199,8 @@ def tile_list_htabg_gate_none_kernel(
                         rhs=h_codes[:, lo:hi].bitcast(FP8X4), rhs_scale=h_scales[:, lo:hi],
                         start=True, stop=True,
                     )
-                ysb = ystage.tile([P, 2, CH], F32, name="ysb")
-                if c == J // CH - 1 and u == 1:
+                ysb = ystage.tile([P, 2, hi - lo], F32, name="ysb")
+                if hi == J and u == 1:
                     nc.vector.tensor_copy(out=ysb[:], in_=yacc[:])
                 else:
                     nc.scalar.copy(out=ysb[:], in_=yacc[:])
@@ -201,21 +208,28 @@ def tile_list_htabg_gate_none_kernel(
 
         last_plane(0)
         last_plane(1)
+        wd_bf = sb("wd_bf", [P, N * PACK], BF16, tag="picked10")
+        nc.scalar.copy(
+            out=wd_bf[:].rearrange("p (c e i) -> p c i e", e=4, i=PACK),
+            in_=wd_raw[:].rearrange("p i (c e) -> p c i e", e=4),
+        )
         last_plane(2)
         quant_x(0)
         last_plane(3)
         quant_x(1)
         gated(0)
         gated(1)
-        quant_x(2)
         gated(2)
-        second(0)
+        nc.vector.quantize_mx(out=wd_codes[:].bitcast(FP8X4), scales=wd_scales[:], in_=wd_bf[:])
+        second(0, 256)
         gated(3)
+        quant_x(2)
+        second(256, 512)
         quant_x(3)
         gated(4)
-        second(1)
         gated(5)
         gated(6)
-        second(2)
+        second(512, 768)
         gated(7)
-        second(3)
+        second(768, 896)
+        second(896, 1024)

@@ -2,6 +2,7 @@ import math
 from contextlib import ExitStack
 
 import concourse.mybir as mybir
+from concourse.masks import make_identity
 
 K, L, R, N, T, J = 512, 512, 512, 512, 2048, 1024
 FLOPS = 2 * J * (K * R + L * R + R * N)
@@ -40,12 +41,23 @@ def tile_list_htabg_gate_none_kernel(
 
         tab_list = keep.tile([P, J // GROUP], U16, name="tab_list")
         head_lists = keep.tile([P, J // GROUP], U16, name="head_lists")
-        tab_w = sb("tab_w", [P, T], I32)
-        wa_w_raw = sb("wa_w_raw", [P, R // 2], I32)
         tab_s = sb("tab_s", [P, T // 4], I32)
-        late_shapes = [("wb_raw", [P, PACK, R], F32), ("wa_s_raw", [P, R // 4], I32),
-                       ("wgt", [P, J], F32), ("wd_raw", [P, PACK, N], F32)]
-        late_shapes += [("plane%d" % i, [P, T], F32) for i in range(PACK)]
+        x_planes = xT.rearrange("(p i) t -> i p t", i=PACK)
+
+        def load_scales(queue, dst, src):
+            for r in range(4):
+                queue.dma_start(out=dst[r:P:32, :], in_=src[0, r:16:4, :].bitcast(I32))
+
+        lt = {name: sb(name, shape, dtype) for name, shape, dtype in [("wgt_rows", [P, P], F32), ("wb_raw", [P, PACK, R], F32)]}
+        late_shapes = [("wa_w_raw", [P, R // 2], I32),
+                       ("tab_w", [P, T], I32),
+                       ("plane0", [P, T], F32),
+                       ("plane1", [P, T], F32),
+                       ("plane2", [P, T], F32),
+                       ("plane3", [P, T], F32),
+                       ("wa_s_raw", [P, R // 4], I32),
+                       ("wd_raw0", [P, PACK, N // 2], F32),
+                       ("wd_raw1", [P, PACK, N // 2], F32)]
         late_at = {}
         words = 0
         for name, shape, dtype in late_shapes:
@@ -54,29 +66,40 @@ def tile_list_htabg_gate_none_kernel(
         warm = late.tile([P, words], F32, name="warm", align_bytes=64, offset=0)
         nc.vector.memset(tab_s[:], 0)
         nc.vector.memset(warm[:, 0:1], 0.0)
-        nc.scalar.activation(warm[:, 1:2], warm[:, 0:1], SIGMOID)
-        lt = {name: late.tile(shape, dtype, name=name, align_bytes=64, offset=late_at[name]) for name, shape, dtype in late_shapes}
-        wb_raw, wa_s_raw, wgt, wd_raw = lt["wb_raw"], lt["wa_s_raw"], lt["wgt"], lt["wd_raw"]
-        planes = [lt["plane%d" % i] for i in range(PACK)]
-        nc.vector.memset(wa_s_raw[:], 0)
-
-        x_planes = xT.rearrange("(p i) t -> i p t", i=PACK)
-
-        def load_scales(queue, dst, src):
-            for q in range(4):
-                queue.dma_start(out=dst[32 * q : 32 * q + 4, :], in_=src[0, 4 * q : 4 * q + 4, :].bitcast(I32))
-
         nc.sync.dma_start(tab_list[:], offs)
+        nc.sync.dma_start(out=lt["wgt_rows"][:], in_=wgt2[0:P:8, :].rearrange("a (c x) -> a c x", x=P))
         nc.sync.dma_start(head_lists[:], offs2)
-        nc.sync.dma_start(out=wa_w_raw[:], in_=wa_words[0].bitcast(I32))
-        nc.sync.dma_start(out=tab_w[:], in_=tab_words[0].rearrange("p t i -> p (t i)").bitcast(I32))
-        load_scales(nc.sync, tab_s, tab_scales)
-        nc.sync.dma_start(out=wb_raw[:], in_=wb.rearrange("(p i) r -> p i r", i=PACK))
-        load_scales(nc.sync, wa_s_raw, wa_scales)
-        nc.sync.dma_start(out=wgt[:], in_=wgt2)
-        for i in range(PACK):
-            nc.sync.dma_start(out=planes[i][:], in_=x_planes[i])
-        nc.sync.dma_start(out=wd_raw[:], in_=wd.rearrange("(p i) n -> p i n", i=PACK))
+        nc.sync.dma_start(out=lt["wb_raw"][:], in_=wb.rearrange("(p i) r -> p i r", i=PACK))
+        load_scales(nc.scalar, tab_s, tab_scales)
+        nc.scalar.activation(warm[:, 1:2], warm[:, 0:1], SIGMOID)
+        for name, shape, dtype in late_shapes:
+            lt[name] = late.tile(shape, dtype, name=name, align_bytes=64, offset=late_at[name])
+        nc.vector.memset(lt["wa_s_raw"][:], 0)
+        nc.sync.dma_start(out=lt["wa_w_raw"][:], in_=wa_words[0].bitcast(I32))
+        nc.sync.dma_start(out=lt["tab_w"][:], in_=tab_words[0].rearrange("p t i -> p (t i)").bitcast(I32))
+        nc.sync.dma_start(out=lt["plane0"][:], in_=x_planes[0])
+        nc.sync.dma_start(out=lt["plane1"][:], in_=x_planes[1])
+        nc.sync.dma_start(out=lt["plane2"][:], in_=x_planes[2])
+        nc.sync.dma_start(out=lt["plane3"][:], in_=x_planes[3])
+        load_scales(nc.sync, lt["wa_s_raw"], wa_scales)
+        nc.sync.dma_start(out=lt["wd_raw0"][:], in_=wd.rearrange("(p i) n -> p i n", i=PACK)[:, :, 0 * N // 2 : 1 * N // 2])
+        nc.sync.dma_start(out=lt["wd_raw1"][:], in_=wd.rearrange("(p i) n -> p i n", i=PACK)[:, :, 1 * N // 2 : 2 * N // 2])
+        tab_w, wa_w_raw, wa_s_raw, wb_raw = lt["tab_w"], lt["wa_w_raw"], lt["wa_s_raw"], lt["wb_raw"]
+        wd_raw = [lt["wd_raw0"], lt["wd_raw1"]]
+        planes = [lt["plane%d" % i] for i in range(PACK)]
+
+        ident = sb("ident", [P, P], F32)
+        make_identity(nc, ident[:])
+        turned = ps2.tile([P, P], F32, name="turned", tag="yacc")
+        nc.tensor.transpose(turned[:], lt["wgt_rows"][:], ident[:])
+        spread = sb("spread", [P, 8, 16, 8], F32)
+        nc.scalar.copy(out=spread[:], in_=turned[:].rearrange("p (a c) -> p c a", c=8).unsqueeze(3).to_broadcast([P, 8, 16, 8]))
+        wgt = sb("wgt", [P, J], F32)
+        for u in range(2):
+            back = ps2.tile([P, 4, P], F32, name="back", tag="yacc")
+            for c in range(4):
+                nc.tensor.transpose(back[:, c, :], spread[:, 4 * u + c].rearrange("p a r -> p (a r)"), ident[:])
+            nc.scalar.copy(out=wgt[:, u * 512 : (u + 1) * 512], in_=back[:].rearrange("p c x -> p (c x)"))
 
         wa_codes = sb("wa_codes", [P, 2 * R], U8)
         wa_sc = sb("wa_sc", [P, R], U8)
@@ -87,24 +110,26 @@ def tile_list_htabg_gate_none_kernel(
 
         v_codes = sb("v_codes", [P, J], U32)
         v_scales = sb("v_scales", [P, J], U8)
-        nc.vector.tensor_copy(v_codes[:], tab_w[:].bitcast(U32).indirect(tab_list[:]))
         nc.vector.tensor_copy(v_scales[:], tab_s[:].bitcast(U8).indirect(tab_list[:]))
 
         wb_bf = sb("wb_bf", [P, R * PACK], BF16)
         wb_codes = sb("wb_codes", [P, R], U32)
         wb_scales = sb("wb_scales", [P, R], U8)
-        nc.scalar.copy(
-            out=wb_bf[:].rearrange("p (t m i) -> p m t i", t=PACK, i=PACK),
-            in_=wb_raw[:].rearrange("p i (m t) -> p m t i", t=PACK),
-        )
+        wb_out = wb_bf[:].rearrange("p (t m i) -> p m t i", t=PACK, i=PACK)
+        wb_in = wb_raw[:].rearrange("p i (m t) -> p m t i", t=PACK)
+        nc.scalar.copy(out=wb_out, in_=wb_in)
 
         nc.vector.quantize_mx(out=wb_codes[:].bitcast(FP8X4), scales=wb_scales[:], in_=wb_bf[:])
-        nc.vector.tensor_copy(
-            out=wa_sc[:].rearrange("p (t m) -> p t m", t=PACK),
-            in_=wa_s_raw[:].bitcast(U8).rearrange("p (m t) -> p t m", t=PACK),
-        )
+        for c in range(J // CH):
+            nc.vector.tensor_copy(
+                v_codes[:, c * CH : (c + 1) * CH],
+                tab_w[:].bitcast(U32).indirect(tab_list[:, c * CH // GROUP : (c + 1) * CH // GROUP]),
+            )
 
-        gate = sb("gate", [P, J, PACK], F32)
+        GATE = J + 2 * CH
+        work = sb("work", [P, GATE + J * PACK], F32)
+        gate = work[:, GATE:].rearrange("p (j t) -> p j t", t=PACK)
+        last_at = [J, J + CH, J, GATE]
         for b in range(J // NB):
             cols = slice(b * NB, (b + 1) * NB)
             acc = ps1.tile([P, PACK, NB], F32, name="acc")
@@ -119,37 +144,34 @@ def tile_list_htabg_gate_none_kernel(
             nc.scalar.activation(gate[:, cols, :], acc[:].rearrange("p t n -> p n t"), SIGMOID)
 
         half = J // 2
-        picked = {
-            (0, 0): sb("picked00", [P, 2, half], F32, tag="wb_bf"),
-            (0, 1): sb("picked01", [P, 2, half], F32),
-            (1, 0): sb("picked10", [P, 2, half], F32),
-            (1, 1): sb("picked11", [P, 2, half], F32),
-        }
+        picked = {}
 
         def gather(i, lo, hi):
-            base = lo // half * half
-            nc.vector.tensor_tensor(
-                picked[i // 2, lo // half][:, i % 2, lo - base : hi - base],
-                planes[i][:].indirect(head_lists[:, lo // GROUP : hi // GROUP]),
-                wgt[:, lo:hi],
-                MULT,
-            )
+            if i == 0:
+                picked[lo] = sb("picked01_%d" % lo, [P, 2, hi - lo], F32)
+            if i < 2:
+                dst = picked[lo][:, i, :]
+            else:
+                at = lo if i == 2 else last_at[lo // CH]
+                dst = work[:, at : at + hi - lo]
+            nc.vector.tensor_tensor(dst, planes[i][:].indirect(head_lists[:, lo // GROUP : hi // GROUP]), wgt[:, lo:hi], MULT)
 
         def lay_pair(i, lo, hi):
-            base = lo // half * half
-            nc.scalar.copy(
-                out=x_bf[:, lo:hi, i : i + 2],
-                in_=picked[i // 2, lo // half][:, :, lo - base : hi - base].rearrange("p i j -> p j i"),
-            )
+            if i == 0:
+                src = picked[lo][:]
+            else:
+                step = last_at[lo // CH] - lo
+                src = work[:, lo : lo + 2 * step].rearrange("p (i x) -> p i x", i=2)[:, :, 0 : hi - lo]
+            nc.scalar.copy(out=x_bf[:, lo:hi, i : i + 2], in_=src.rearrange("p i j -> p j i"))
 
         for i in range(2):
-            gather(i, 0, J // 2)
-            gather(i, J // 2, J)
+            gather(i, 0, half)
+            gather(i, half, J)
         x_bf = sb("x_bf", [P, J, PACK], BF16, tag="wb_codes")
-        lay_pair(0, 0, J // 2)
-        lay_pair(0, J // 2, J)
-        gather(2, 0, J // 2)
-        gather(2, J // 2, J)
+        lay_pair(0, 0, half)
+        lay_pair(0, half, J)
+        gather(2, 0, half)
+        gather(2, half, J)
 
         wd_codes = sb("wd_codes", [P, N], U32)
         wd_scales = sb("wd_scales", [P, N], U8)
@@ -167,6 +189,12 @@ def tile_list_htabg_gate_none_kernel(
                 in_=src[:, lo:hi, :].rearrange("p j i -> p (j i)"),
             )
 
+        def lay_wa_scales():
+            nc.vector.tensor_copy(
+                out=wa_sc[:].rearrange("p (t m) -> p t m", t=PACK),
+                in_=wa_s_raw[:].bitcast(U8).rearrange("p (m t) -> p t m", t=PACK),
+            )
+
         def last_plane(c):
             gather(3, c * CH, (c + 1) * CH)
             lay_pair(2, c * CH, (c + 1) * CH)
@@ -174,9 +202,12 @@ def tile_list_htabg_gate_none_kernel(
         def quant_x(c):
             quant(x_codes, x_scales, x_bf, c * CH, (c + 1) * CH)
 
-        def gated(b):
+        ya = [None] * (J // NB)
+
+        def first(b):
             cols = slice(b * NB, (b + 1) * NB)
             acc = ps1.tile([P, PACK, NB], F32, name="acc")
+            ya[b] = acc
             for t in range(PACK):
                 nc.tensor.matmul_mx(
                     out=acc[:, t, :],
@@ -185,11 +216,26 @@ def tile_list_htabg_gate_none_kernel(
                     rhs=x_codes[:, cols].bitcast(FP8X4), rhs_scale=x_scales[:, cols],
                     start=True, stop=True,
                 )
-            nc.vector.tensor_tensor(h_bf[:, cols, :], acc[:].rearrange("p t n -> p n t"), gate[:, cols, :], MULT)
 
-        def second(lo, hi):
+        def gated(b):
+            cols = slice(b * NB, (b + 1) * NB)
+            nc.vector.tensor_tensor(h_bf[:, cols, :], ya[b][:].rearrange("p t n -> p n t"), gate[:, cols, :], MULT)
+
+        def quant_h(lo, hi):
             quant(h_codes, h_scales, h_bf, lo, hi)
-            for u in range(2):
+
+        def lay_wd(u):
+            nc.scalar.copy(
+                out=wd_bf[u][:].rearrange("p (c e i) -> p c i e", e=4, i=PACK),
+                in_=wd_raw[u][:].rearrange("p i (c e) -> p c i e", e=4),
+            )
+
+        def quant_wd(u):
+            cols = slice(u * N // 2, (u + 1) * N // 2)
+            nc.vector.quantize_mx(out=wd_codes[:, cols].bitcast(FP8X4), scales=wd_scales[:, cols], in_=wd_bf[u][:])
+
+        def second(lo, hi, halves, on_vector=()):
+            for u in halves:
                 yacc = ps2.tile([P, 2, hi - lo], F32, name="yacc")
                 for a in range(2):
                     m = slice((2 * u + a) * P, (2 * u + a + 1) * P)
@@ -200,36 +246,50 @@ def tile_list_htabg_gate_none_kernel(
                         start=True, stop=True,
                     )
                 ysb = ystage.tile([P, 2, hi - lo], F32, name="ysb")
-                if hi == J and u == 1:
+                if u in on_vector:
                     nc.vector.tensor_copy(out=ysb[:], in_=yacc[:])
                 else:
                     nc.scalar.copy(out=ysb[:], in_=yacc[:])
                 nc.sync.dma_start(out=out_v[:, 2 * u : 2 * u + 2, lo:hi], in_=ysb[:])
 
+        wd_bf = [sb("wd_bf%d" % u, [P, N * PACK // 2], BF16) for u in range(2)]
         last_plane(0)
         last_plane(1)
-        wd_bf = sb("wd_bf", [P, N * PACK], BF16, tag="picked10")
-        nc.scalar.copy(
-            out=wd_bf[:].rearrange("p (c e i) -> p c i e", e=4, i=PACK),
-            in_=wd_raw[:].rearrange("p i (c e) -> p c i e", e=4),
-        )
-        last_plane(2)
+        lay_wa_scales()
+        lay_wd(0)
         quant_x(0)
-        last_plane(3)
+        first(0)
+        first(1)
+        last_plane(2)
         quant_x(1)
+        first(2)
+        first(3)
+        lay_wd(1)
         gated(0)
         gated(1)
-        gated(2)
-        nc.vector.quantize_mx(out=wd_codes[:].bitcast(FP8X4), scales=wd_scales[:], in_=wd_bf[:])
-        second(0, 256)
-        gated(3)
+        quant_wd(0)
+        quant_h(0,256)
+        second(0,256,[0])
+        last_plane(3)
         quant_x(2)
-        second(256, 512)
+        first(4)
+        first(5)
+        gated(2)
+        quant_wd(1)
+        second(0,256,[1])
+        gated(3)
         quant_x(3)
+        first(6)
+        first(7)
+        quant_h(256,512)
+        second(256,512,[0,1])
         gated(4)
         gated(5)
         gated(6)
-        second(512, 768)
+        quant_h(512,768)
+        second(512,768,[0,1])
         gated(7)
-        second(768, 896)
-        second(896, 1024)
+        quant_h(768,896)
+        quant_h(896,1024)
+        second(768,896,[0,1],[1])
+        second(896,1024,[0,1],[1])

@@ -128,7 +128,7 @@ def tile_list_htabg_gate_none_kernel(
 
         GATE = J + 2 * CH
         work = sb("work", [P, GATE + J * PACK], F32)
-        gate = work[:, GATE:].rearrange("p (j t) -> p j t", t=PACK)
+        gate = work[:, GATE:].rearrange("p (b t n) -> p b t n", t=PACK, n=NB)
         last_at = [J, J + CH, J, GATE]
         for b in range(J // NB):
             cols = slice(b * NB, (b + 1) * NB)
@@ -141,7 +141,7 @@ def tile_list_htabg_gate_none_kernel(
                     rhs=v_codes[:, cols].bitcast(FP8X4), rhs_scale=v_scales[:, cols],
                     start=True, stop=True,
                 )
-            nc.scalar.activation(gate[:, cols, :], acc[:].rearrange("p t n -> p n t"), SIGMOID)
+            nc.scalar.activation(gate[:, b], acc[:], SIGMOID)
 
         half = J // 2
         picked = {}
@@ -219,7 +219,12 @@ def tile_list_htabg_gate_none_kernel(
 
         def gated(b):
             cols = slice(b * NB, (b + 1) * NB)
-            nc.vector.tensor_tensor(h_bf[:, cols, :], ya[b][:].rearrange("p t n -> p n t"), gate[:, cols, :], MULT)
+            nc.vector.tensor_tensor(
+                h_bf[:, cols, :].rearrange("p (c e) t -> p c t e", e=4),
+                ya[b][:].rearrange("p t (c e) -> p c t e", e=4),
+                gate[:, b].rearrange("p t (c e) -> p c t e", e=4),
+                MULT,
+            )
 
         def quant_h(lo, hi):
             quant(h_codes, h_scales, h_bf, lo, hi)

@@ -48,14 +48,14 @@ def tile_list_htabg_gate_none_kernel(
             for r in range(4):
                 queue.dma_start(out=dst[r:P:32, :], in_=src[0, r:16:4, :].bitcast(I32))
 
-        lt = {name: sb(name, shape, dtype) for name, shape, dtype in [("wgt_rows", [P, P], F32), ("wb_raw", [P, PACK, R], F32)]}
+        lt = {name: sb(name, shape, dtype) for name, shape, dtype in [("wb_raw", [P, PACK, R], F32)]}
         late_shapes = [("wa_w_raw", [P, R // 2], I32),
                        ("tab_w", [P, T], I32),
+                       ("wa_s_raw", [P, R // 4], I32),
                        ("plane0", [P, T], F32),
                        ("plane1", [P, T], F32),
                        ("plane2", [P, T], F32),
                        ("plane3", [P, T], F32),
-                       ("wa_s_raw", [P, R // 4], I32),
                        ("wd_raw0", [P, PACK, N // 2], F32),
                        ("wd_raw1", [P, PACK, N // 2], F32)]
         late_at = {}
@@ -63,43 +63,39 @@ def tile_list_htabg_gate_none_kernel(
         for name, shape, dtype in late_shapes:
             late_at[name] = 4 * words
             words += math.prod(shape[1:])
-        warm = late.tile([P, words], F32, name="warm", align_bytes=64, offset=0)
-        nc.vector.memset(tab_s[:], 0)
-        nc.vector.memset(warm[:, 0:1], 0.0)
+        rows_span = late.tile([P, words], F32, name="wgt_rows", align_bytes=64, offset=0)
+        wgt_rows = rows_span[:, 0:P]
+        warm = sb("warm", [P, 2], F32)
+        nc.gpsimd.memset(tab_s[:], 0)
+        nc.gpsimd.memset(warm[:, 0:1], 0.0)
+        nc.sync.dma_start(out=wgt_rows, in_=wgt2[0:P:8, :].rearrange("a (c x) -> a c x", x=P))
         nc.sync.dma_start(tab_list[:], offs)
-        nc.sync.dma_start(out=lt["wgt_rows"][:], in_=wgt2[0:P:8, :].rearrange("a (c x) -> a c x", x=P))
         nc.sync.dma_start(head_lists[:], offs2)
         nc.sync.dma_start(out=lt["wb_raw"][:], in_=wb.rearrange("(p i) r -> p i r", i=PACK))
         load_scales(nc.scalar, tab_s, tab_scales)
         nc.scalar.activation(warm[:, 1:2], warm[:, 0:1], SIGMOID)
+        ident = sb("ident", [P, P], F32)
+        make_identity(nc, ident[:])
+        turned = ps2.tile([P, P], F32, name="turned", tag="yacc")
+        nc.tensor.transpose(turned[:], wgt_rows, ident[:])
         for name, shape, dtype in late_shapes:
             lt[name] = late.tile(shape, dtype, name=name, align_bytes=64, offset=late_at[name])
-        nc.vector.memset(lt["wa_s_raw"][:], 0)
+        nc.gpsimd.memset(lt["wa_s_raw"][:], 0)
         nc.sync.dma_start(out=lt["wa_w_raw"][:], in_=wa_words[0].bitcast(I32))
         nc.sync.dma_start(out=lt["tab_w"][:], in_=tab_words[0].rearrange("p t i -> p (t i)").bitcast(I32))
+        load_scales(nc.sync, lt["wa_s_raw"], wa_scales)
         nc.sync.dma_start(out=lt["plane0"][:], in_=x_planes[0])
         nc.sync.dma_start(out=lt["plane1"][:], in_=x_planes[1])
         nc.sync.dma_start(out=lt["plane2"][:], in_=x_planes[2])
         nc.sync.dma_start(out=lt["plane3"][:], in_=x_planes[3])
-        load_scales(nc.sync, lt["wa_s_raw"], wa_scales)
         nc.sync.dma_start(out=lt["wd_raw0"][:], in_=wd.rearrange("(p i) n -> p i n", i=PACK)[:, :, 0 * N // 2 : 1 * N // 2])
         nc.sync.dma_start(out=lt["wd_raw1"][:], in_=wd.rearrange("(p i) n -> p i n", i=PACK)[:, :, 1 * N // 2 : 2 * N // 2])
         tab_w, wa_w_raw, wa_s_raw, wb_raw = lt["tab_w"], lt["wa_w_raw"], lt["wa_s_raw"], lt["wb_raw"]
         wd_raw = [lt["wd_raw0"], lt["wd_raw1"]]
         planes = [lt["plane%d" % i] for i in range(PACK)]
 
-        ident = sb("ident", [P, P], F32)
-        make_identity(nc, ident[:])
-        turned = ps2.tile([P, P], F32, name="turned", tag="yacc")
-        nc.tensor.transpose(turned[:], lt["wgt_rows"][:], ident[:])
         spread = sb("spread", [P, 8, 16, 8], F32)
         nc.scalar.copy(out=spread[:], in_=turned[:].rearrange("p (a c) -> p c a", c=8).unsqueeze(3).to_broadcast([P, 8, 16, 8]))
-        wgt = sb("wgt", [P, J], F32)
-        for u in range(2):
-            back = ps2.tile([P, 4, P], F32, name="back", tag="yacc")
-            for c in range(4):
-                nc.tensor.transpose(back[:, c, :], spread[:, 4 * u + c].rearrange("p a r -> p (a r)"), ident[:])
-            nc.scalar.copy(out=wgt[:, u * 512 : (u + 1) * 512], in_=back[:].rearrange("p c x -> p (c x)"))
 
         wa_codes = sb("wa_codes", [P, 2 * R], U8)
         wa_sc = sb("wa_sc", [P, R], U8)
@@ -112,24 +108,28 @@ def tile_list_htabg_gate_none_kernel(
         v_scales = sb("v_scales", [P, J], U8)
         nc.vector.tensor_copy(v_scales[:], tab_s[:].bitcast(U8).indirect(tab_list[:]))
 
-        wb_bf = sb("wb_bf", [P, R * PACK], BF16)
+        wb_bf = [sb("wb_bf0", [P, R * PACK // 2], BF16), sb("wb_bf1", [P, R * PACK // 2], BF16, tag="tab_s")]
         wb_codes = sb("wb_codes", [P, R], U32)
         wb_scales = sb("wb_scales", [P, R], U8)
-        wb_out = wb_bf[:].rearrange("p (t m i) -> p m t i", t=PACK, i=PACK)
         wb_in = wb_raw[:].rearrange("p i (m t) -> p m t i", t=PACK)
-        nc.scalar.copy(out=wb_out, in_=wb_in)
-
-        nc.vector.quantize_mx(out=wb_codes[:].bitcast(FP8X4), scales=wb_scales[:], in_=wb_bf[:])
+        for u, copy in enumerate((nc.scalar.copy, nc.vector.tensor_copy)):
+            copy(out=wb_bf[u][:].rearrange("p (t m i) -> p m t i", t=2, i=PACK), in_=wb_in[:, :, 2 * u : 2 * u + 2])
+        for u in (1, 0):
+            cols = slice(u * R // 2, (u + 1) * R // 2)
+            nc.vector.quantize_mx(out=wb_codes[:, cols].bitcast(FP8X4), scales=wb_scales[:, cols], in_=wb_bf[u][:])
+        wgt = sb("wgt", [P, J], F32)
+        for u in range(2):
+            back = ps2.tile([P, 4, P], F32, name="back", tag="yacc")
+            for c in range(4):
+                nc.tensor.transpose(back[:, c, :], spread[:, 4 * u + c].rearrange("p a r -> p (a r)"), ident[:])
+            nc.scalar.copy(out=wgt[:, u * 512 : (u + 1) * 512], in_=back[:].rearrange("p c x -> p (c x)"))
         for c in range(J // CH):
             nc.vector.tensor_copy(
                 v_codes[:, c * CH : (c + 1) * CH],
                 tab_w[:].bitcast(U32).indirect(tab_list[:, c * CH // GROUP : (c + 1) * CH // GROUP]),
             )
 
-        GATE = J + 2 * CH
-        work = sb("work", [P, GATE + J * PACK], F32)
-        gate = work[:, GATE:].rearrange("p (b t n) -> p b t n", t=PACK, n=NB)
-        last_at = [J, J + CH, J, GATE]
+        gate = sb("gate", [P, J // NB, PACK, NB], F32)
         for b in range(J // NB):
             cols = slice(b * NB, (b + 1) * NB)
             acc = ps1.tile([P, PACK, NB], F32, name="acc")
@@ -147,22 +147,20 @@ def tile_list_htabg_gate_none_kernel(
         picked = {}
 
         def gather(i, lo, hi):
-            if i == 0:
-                picked[lo] = sb("picked01_%d" % lo, [P, 2, hi - lo], F32)
-            if i < 2:
-                dst = picked[lo][:, i, :]
-            else:
-                at = lo if i == 2 else last_at[lo // CH]
-                dst = work[:, at : at + hi - lo]
-            nc.vector.tensor_tensor(dst, planes[i][:].indirect(head_lists[:, lo // GROUP : hi // GROUP]), wgt[:, lo:hi], MULT)
+            if i % 2 == 0:
+                if i == 0:
+                    picked[0, lo] = sb("picked01_%d" % lo, [P, 2, hi - lo], F32)
+                else:
+                    picked[1, lo] = keep.tile([P, 2, hi - lo], F32, name="picked23", align_bytes=64, bufs=3)
+            nc.vector.tensor_tensor(
+                picked[i // 2, lo][:, i % 2, :],
+                planes[i][:].indirect(head_lists[:, lo // GROUP : hi // GROUP]),
+                wgt[:, lo:hi],
+                MULT,
+            )
 
         def lay_pair(i, lo, hi):
-            if i == 0:
-                src = picked[lo][:]
-            else:
-                step = last_at[lo // CH] - lo
-                src = work[:, lo : lo + 2 * step].rearrange("p (i x) -> p i x", i=2)[:, :, 0 : hi - lo]
-            nc.scalar.copy(out=x_bf[:, lo:hi, i : i + 2], in_=src.rearrange("p i j -> p j i"))
+            nc.scalar.copy(out=x_bf[:, lo:hi, i : i + 2], in_=picked[i // 2, lo][:].rearrange("p i j -> p j i"))
 
         for i in range(2):
             gather(i, 0, half)
@@ -170,8 +168,8 @@ def tile_list_htabg_gate_none_kernel(
         x_bf = sb("x_bf", [P, J, PACK], BF16, tag="wb_codes")
         lay_pair(0, 0, half)
         lay_pair(0, half, J)
-        gather(2, 0, half)
-        gather(2, half, J)
+        for c in range(3):
+            gather(2, c * CH, (c + 1) * CH)
 
         wd_codes = sb("wd_codes", [P, N], U32)
         wd_scales = sb("wd_scales", [P, N], U8)
@@ -196,6 +194,8 @@ def tile_list_htabg_gate_none_kernel(
             )
 
         def last_plane(c):
+            if c >= 3:
+                gather(2, c * CH, (c + 1) * CH)
             gather(3, c * CH, (c + 1) * CH)
             lay_pair(2, c * CH, (c + 1) * CH)
 
@@ -258,14 +258,15 @@ def tile_list_htabg_gate_none_kernel(
                 nc.sync.dma_start(out=out_v[:, 2 * u : 2 * u + 2, lo:hi], in_=ysb[:])
 
         wd_bf = [sb("wd_bf%d" % u, [P, N * PACK // 2], BF16) for u in range(2)]
+        lay_wa_scales()
         last_plane(0)
         last_plane(1)
-        lay_wa_scales()
         lay_wd(0)
+        last_plane(2)
         quant_x(0)
         first(0)
         first(1)
-        last_plane(2)
+        last_plane(3)
         quant_x(1)
         first(2)
         first(3)
@@ -275,26 +276,27 @@ def tile_list_htabg_gate_none_kernel(
         quant_wd(0)
         quant_h(0,256)
         second(0,256,[0])
-        last_plane(3)
+        gated(2)
         quant_x(2)
         first(4)
         first(5)
-        gated(2)
-        quant_wd(1)
-        second(0,256,[1])
         gated(3)
+        quant_wd(1)
+        quant_h(256,512)
+        second(256,512,[0])
+        second(0,256,[1])
+        second(256,512,[1])
+        gated(4)
         quant_x(3)
         first(6)
         first(7)
-        quant_h(256,512)
-        second(256,512,[0,1])
-        gated(4)
         gated(5)
-        gated(6)
-        quant_h(512,768)
+        quant_h(512,640)
+        quant_h(640,768)
         second(512,768,[0,1])
-        gated(7)
+        gated(6)
         quant_h(768,896)
+        gated(7)
+        second(768,896,[0,1])
         quant_h(896,1024)
-        second(768,896,[0,1],[1])
         second(896,1024,[0,1],[1])

@@ -71,8 +71,8 @@ def tile_list_htabg_gate_none_kernel(
         nc.sync.dma_start(out=wgt_rows, in_=wgt2[0:P:8, :].rearrange("a (c x) -> a c x", x=P))
         nc.sync.dma_start(tab_list[:], offs)
         nc.sync.dma_start(head_lists[:], offs2)
+        load_scales(nc.sync, tab_s, tab_scales)
         nc.sync.dma_start(out=lt["wb_raw"][:], in_=wb.rearrange("(p i) r -> p i r", i=PACK))
-        load_scales(nc.scalar, tab_s, tab_scales)
         nc.scalar.activation(warm[:, 1:2], warm[:, 0:1], SIGMOID)
         ident = sb("ident", [P, P], F32)
         make_identity(nc, ident[:])
@@ -117,7 +117,7 @@ def tile_list_htabg_gate_none_kernel(
         for u in (1, 0):
             cols = slice(u * R // 2, (u + 1) * R // 2)
             nc.vector.quantize_mx(out=wb_codes[:, cols].bitcast(FP8X4), scales=wb_scales[:, cols], in_=wb_bf[u][:])
-        wgt = sb("wgt", [P, J], F32)
+        wgt = sb("wgt", [P, J], F32, tag="wb_raw")
         for u in range(2):
             back = ps2.tile([P, 4, P], F32, name="back", tag="yacc")
             for c in range(4):

@@ -257,6 +257,21 @@ def tile_list_htabg_gate_none_kernel(
                     nc.scalar.copy(out=ysb[:], in_=yacc[:])
                 nc.sync.dma_start(out=out_v[:, 2 * u : 2 * u + 2, lo:hi], in_=ysb[:])
 
+        def second_block(b):
+            cols = slice(b * NB, (b + 1) * NB)
+            yacc = ps2.tile([P, PACK, NB], F32, name="yacc")
+            for a in range(PACK):
+                m = slice(a * P, (a + 1) * P)
+                nc.tensor.matmul_mx(
+                    out=yacc[:, a, :],
+                    lhsT=wd_codes[:, m].bitcast(FP8X4), lhsT_scale=wd_scales[:, m],
+                    rhs=h_codes[:, cols].bitcast(FP8X4), rhs_scale=h_scales[:, cols],
+                    start=True, stop=True,
+                )
+            ysb = ystage.tile([P, PACK, NB], F32, name="ysb")
+            nc.scalar.copy(out=ysb[:], in_=yacc[:])
+            nc.sync.dma_start(out=out_v[:, :, cols], in_=ysb[:])
+
         wd_bf = [sb("wd_bf%d" % u, [P, N * PACK // 2], BF16) for u in range(2)]
         lay_wa_scales()
         last_plane(0)
@@ -267,36 +282,36 @@ def tile_list_htabg_gate_none_kernel(
         first(0)
         first(1)
         last_plane(3)
+        lay_wd(1)
         quant_x(1)
         first(2)
         first(3)
-        lay_wd(1)
         gated(0)
-        gated(1)
         quant_wd(0)
-        quant_h(0,256)
-        second(0,256,[0])
-        gated(2)
+        gated(1)
         quant_x(2)
         first(4)
         first(5)
-        gated(3)
-        quant_wd(1)
-        quant_h(256,512)
-        second(256,512,[0])
-        second(0,256,[1])
-        second(256,512,[1])
-        gated(4)
+        quant_h(0, 256)
+        second(0, 256, [0])
+        gated(2)
         quant_x(3)
+        gated(3)
         first(6)
         first(7)
+        quant_wd(1)
+        second(0, 256, [1])
+        quant_h(256, 512)
+        second(256, 512, [0, 1])
+        gated(4)
         gated(5)
-        quant_h(512,640)
-        quant_h(640,768)
-        second(512,768,[0,1])
+        quant_h(512, 640)
+        second_block(4)
         gated(6)
-        quant_h(768,896)
+        quant_h(640, 768)
+        second_block(5)
         gated(7)
-        second(768,896,[0,1])
-        quant_h(896,1024)
-        second(896,1024,[0,1],[1])
+        quant_h(768, 896)
+        quant_h(896, 1024)
+        second(768, 896, [0, 1], [1])
+        second(896, 1024, [0, 1], [1])

@@ -23,6 +23,7 @@ PACK = 4
 GROUP = 16
 NB = 128
 CH = 256
+RUN = 8
 
 
 def tile_list_htabg_gate_none_kernel(
@@ -55,8 +56,8 @@ def tile_list_htabg_gate_none_kernel(
                        ("plane0", [P, T], F32),
                        ("plane1", [P, T], F32),
                        ("plane2", [P, T], F32),
-                       ("plane3", [P, T], F32),
                        ("wd_raw0", [P, PACK, N // 2], F32),
+                       ("plane3", [P, T], F32),
                        ("wd_raw1", [P, PACK, N // 2], F32)]
         late_at = {}
         words = 0
@@ -87,9 +88,15 @@ def tile_list_htabg_gate_none_kernel(
         nc.sync.dma_start(out=lt["plane0"][:], in_=x_planes[0])
         nc.sync.dma_start(out=lt["plane1"][:], in_=x_planes[1])
         nc.sync.dma_start(out=lt["plane2"][:], in_=x_planes[2])
+        wd_rows = wd.rearrange("(q t e) n -> t q e n", t=PACK, e=RUN)
+
+        def load_wd(u):
+            for t in range(PACK):
+                nc.sync.dma_start(out=lt["wd_raw%d" % u][:, t, :], in_=wd_rows[t][:, :, u * N // 2 : (u + 1) * N // 2])
+
+        load_wd(0)
         nc.sync.dma_start(out=lt["plane3"][:], in_=x_planes[3])
-        nc.sync.dma_start(out=lt["wd_raw0"][:], in_=wd.rearrange("(p i) n -> p i n", i=PACK)[:, :, 0 * N // 2 : 1 * N // 2])
-        nc.sync.dma_start(out=lt["wd_raw1"][:], in_=wd.rearrange("(p i) n -> p i n", i=PACK)[:, :, 1 * N // 2 : 2 * N // 2])
+        load_wd(1)
         tab_w, wa_w_raw, wa_s_raw, wb_raw = lt["tab_w"], lt["wa_w_raw"], lt["wa_s_raw"], lt["wb_raw"]
         wd_raw = [lt["wd_raw0"], lt["wd_raw1"]]
         planes = [lt["plane%d" % i] for i in range(PACK)]
@@ -100,8 +107,8 @@ def tile_list_htabg_gate_none_kernel(
         wa_codes = sb("wa_codes", [P, 2 * R], U8)
         wa_sc = sb("wa_sc", [P, R], U8)
         nc.vector.tensor_copy(
-            out=wa_codes[:].bitcast(U16).rearrange("p (t m) -> p t m", t=PACK),
-            in_=wa_w_raw[:].bitcast(U16).rearrange("p (m t) -> p t m", t=PACK),
+            out=wa_codes[:].bitcast(I32).rearrange("p (t q e) -> p t q e", t=PACK, e=RUN // 2),
+            in_=wa_w_raw[:].rearrange("p (q t e) -> p t q e", t=PACK, e=RUN // 2),
         )
 
         v_codes = sb("v_codes", [P, J], U32)
@@ -111,9 +118,14 @@ def tile_list_htabg_gate_none_kernel(
         wb_bf = [sb("wb_bf0", [P, R * PACK // 2], BF16), sb("wb_bf1", [P, R * PACK // 2], BF16, tag="tab_s")]
         wb_codes = sb("wb_codes", [P, R], U32)
         wb_scales = sb("wb_scales", [P, R], U8)
-        wb_in = wb_raw[:].rearrange("p i (m t) -> p m t i", t=PACK)
-        for u, copy in enumerate((nc.scalar.copy, nc.vector.tensor_copy)):
-            copy(out=wb_bf[u][:].rearrange("p (t m i) -> p m t i", t=2, i=PACK), in_=wb_in[:, :, 2 * u : 2 * u + 2])
+        wb_in = wb_raw[:].rearrange("p i (q t d e) -> p t q d i e", t=PACK, d=2, e=4)
+        wb_out = wb_bf[0][:].rearrange("p (t q d e i) -> p t q d i e", t=2, d=2, e=4, i=PACK)
+        for t in range(2):
+            nc.scalar.copy(out=wb_out[:, t], in_=wb_in[:, t])
+        nc.vector.tensor_copy(
+            out=wb_bf[1][:].rearrange("p (t q e i) -> p t q e i", t=2, e=RUN, i=PACK),
+            in_=wb_raw[:].rearrange("p i (q t e) -> p t q e i", t=PACK, e=RUN)[:, 2:4],
+        )
         for u in (1, 0):
             cols = slice(u * R // 2, (u + 1) * R // 2)
             nc.vector.quantize_mx(out=wb_codes[:, cols].bitcast(FP8X4), scales=wb_scales[:, cols], in_=wb_bf[u][:])
@@ -123,13 +135,13 @@ def tile_list_htabg_gate_none_kernel(
             for c in range(4):
                 nc.tensor.transpose(back[:, c, :], spread[:, 4 * u + c].rearrange("p a r -> p (a r)"), ident[:])
             nc.scalar.copy(out=wgt[:, u * 512 : (u + 1) * 512], in_=back[:].rearrange("p c x -> p (c x)"))
-        for c in range(J // CH):
+        for lo, hi in ((0, 256), (256, 512), (512, 1024)):
             nc.vector.tensor_copy(
-                v_codes[:, c * CH : (c + 1) * CH],
-                tab_w[:].bitcast(U32).indirect(tab_list[:, c * CH // GROUP : (c + 1) * CH // GROUP]),
+                v_codes[:, lo:hi],
+                tab_w[:].bitcast(U32).indirect(tab_list[:, lo // GROUP : hi // GROUP]),
             )
 
-        gate = sb("gate", [P, J // NB, PACK, NB], F32)
+        gate = [sb("gate%d" % b, [P, PACK, NB], F32) for b in range(J // NB)]
         for b in range(J // NB):
             cols = slice(b * NB, (b + 1) * NB)
             acc = ps1.tile([P, PACK, NB], F32, name="acc")
@@ -141,37 +153,44 @@ def tile_list_htabg_gate_none_kernel(
                     rhs=v_codes[:, cols].bitcast(FP8X4), rhs_scale=v_scales[:, cols],
                     start=True, stop=True,
                 )
-            nc.scalar.activation(gate[:, b], acc[:], SIGMOID)
+            nc.scalar.activation(gate[b][:], acc[:], SIGMOID)
 
         half = J // 2
-        picked = {}
+        pair01 = sb("pair01", [P, 2, half], F32)
+        shared = sb("shared", [P, 5 * CH], F32)
+        pair23 = [shared[:, 3 * CH : 5 * CH], sb("pair23", [P, 2 * CH], F32)[:]]
+        quad = {2: sb("quad", [P, PACK * CH], F32)[:], 3: shared[:, 0 : PACK * CH]}
 
-        def gather(i, lo, hi):
-            if i % 2 == 0:
-                if i == 0:
-                    picked[0, lo] = sb("picked01_%d" % lo, [P, 2, hi - lo], F32)
-                else:
-                    picked[1, lo] = keep.tile([P, 2, hi - lo], F32, name="picked23", align_bytes=64, bufs=3)
+        def gather(i, lo, hi, dst):
             nc.vector.tensor_tensor(
-                picked[i // 2, lo][:, i % 2, :],
+                dst,
                 planes[i][:].indirect(head_lists[:, lo // GROUP : hi // GROUP]),
                 wgt[:, lo:hi],
                 MULT,
             )
 
-        def lay_pair(i, lo, hi):
-            nc.scalar.copy(out=x_bf[:, lo:hi, i : i + 2], in_=picked[i // 2, lo][:].rearrange("p i j -> p j i"))
+        def lay_pair(i, lo, hi, src):
+            nc.scalar.copy(out=x_bf[:, lo:hi, i : i + 2], in_=src.rearrange("p (i j) -> p j i", i=2))
+
+        def lay_four(c):
+            nc.scalar.copy(
+                out=x_bf[:, c * CH : (c + 1) * CH, :].rearrange("p (c e) i -> p c i e", e=4),
+                in_=quad[c].rearrange("p (i c e) -> p c i e", i=PACK, e=4),
+            )
+
+        def gather_chunk(i, c):
+            dst = quad[c][:, i * CH : (i + 1) * CH] if c >= 2 else pair23[c][:, (i - 2) * CH : (i - 1) * CH]
+            gather(i, c * CH, (c + 1) * CH, dst)
 
         for i in range(2):
-            gather(i, 0, half)
-            gather(i, half, J)
+            gather(i, 0, half, pair01[:, i, :])
+            gather_chunk(i, 2)
+            gather_chunk(i, 3)
         x_bf = sb("x_bf", [P, J, PACK], BF16, tag="wb_codes")
-        lay_pair(0, 0, half)
-        lay_pair(0, half, J)
-        for c in range(3):
-            gather(2, c * CH, (c + 1) * CH)
+        lay_pair(0, 0, half, pair01[:].rearrange("p i j -> p (i j)"))
+        for c in range(4):
+            gather_chunk(2, c)
 
-        wd_codes = sb("wd_codes", [P, N], U32)
         wd_scales = sb("wd_scales", [P, N], U8)
 
         x_codes = sb("x_codes", [P, J], U32)
@@ -189,18 +208,19 @@ def tile_list_htabg_gate_none_kernel(
 
         def lay_wa_scales():
             nc.vector.tensor_copy(
-                out=wa_sc[:].rearrange("p (t m) -> p t m", t=PACK),
-                in_=wa_s_raw[:].bitcast(U8).rearrange("p (m t) -> p t m", t=PACK),
+                out=wa_sc[:].bitcast(I32).rearrange("p (t q e) -> p t q e", t=PACK, e=RUN // 4),
+                in_=wa_s_raw[:].rearrange("p (q t e) -> p t q e", t=PACK, e=RUN // 4),
             )
 
         def last_plane(c):
-            if c >= 3:
-                gather(2, c * CH, (c + 1) * CH)
-            gather(3, c * CH, (c + 1) * CH)
-            lay_pair(2, c * CH, (c + 1) * CH)
+            gather_chunk(3, c)
+            if c < 2:
+                lay_pair(2, c * CH, (c + 1) * CH, pair23[c])
+            else:
+                lay_four(c)
 
-        def quant_x(c):
-            quant(x_codes, x_scales, x_bf, c * CH, (c + 1) * CH)
+        def quant_x(lo, hi):
+            quant(x_codes, x_scales, x_bf, lo, hi)
 
         ya = [None] * (J // NB)
 
@@ -217,12 +237,11 @@ def tile_list_htabg_gate_none_kernel(
                     start=True, stop=True,
                 )
 
-        def gated(b):
-            cols = slice(b * NB, (b + 1) * NB)
+        def gated(b, lo=0, hi=NB):
             nc.vector.tensor_tensor(
-                h_bf[:, cols, :].rearrange("p (c e) t -> p c t e", e=4),
-                ya[b][:].rearrange("p t (c e) -> p c t e", e=4),
-                gate[:, b].rearrange("p t (c e) -> p c t e", e=4),
+                h_bf[:, b * NB + lo : b * NB + hi, :].rearrange("p (c e) t -> p c t e", e=4),
+                ya[b][:, :, lo:hi].rearrange("p t (c e) -> p c t e", e=4),
+                gate[b][:, :, lo:hi].rearrange("p t (c e) -> p c t e", e=4),
                 MULT,
             )
 
@@ -235,18 +254,24 @@ def tile_list_htabg_gate_none_kernel(
                 in_=wd_raw[u][:].rearrange("p i (c e) -> p c i e", e=4),
             )
 
+        wd_codes = []
+
         def quant_wd(u):
             cols = slice(u * N // 2, (u + 1) * N // 2)
-            nc.vector.quantize_mx(out=wd_codes[:, cols].bitcast(FP8X4), scales=wd_scales[:, cols], in_=wd_bf[u][:])
+            wd_codes.append(sb("wd_codes%d" % u, [P, N // 2], U32, tag=("wd_codes0", "gate2")[u]))
+            nc.vector.quantize_mx(out=wd_codes[u][:].bitcast(FP8X4), scales=wd_scales[:, cols], in_=wd_bf[u][:])
 
         def second(lo, hi, halves, on_vector=()):
             for u in halves:
-                yacc = ps2.tile([P, 2, hi - lo], F32, name="yacc")
+                if u in on_vector:
+                    yacc = ps1.tile([P, 2, hi - lo], F32, name="acc")
+                else:
+                    yacc = ps2.tile([P, 2, hi - lo], F32, name="yacc")
                 for a in range(2):
                     m = slice((2 * u + a) * P, (2 * u + a + 1) * P)
                     nc.tensor.matmul_mx(
                         out=yacc[:, a, :],
-                        lhsT=wd_codes[:, m].bitcast(FP8X4), lhsT_scale=wd_scales[:, m],
+                        lhsT=wd_codes[u][:, a * P : (a + 1) * P].bitcast(FP8X4), lhsT_scale=wd_scales[:, m],
                         rhs=h_codes[:, lo:hi].bitcast(FP8X4), rhs_scale=h_scales[:, lo:hi],
                         start=True, stop=True,
                     )
@@ -264,7 +289,7 @@ def tile_list_htabg_gate_none_kernel(
                 m = slice(a * P, (a + 1) * P)
                 nc.tensor.matmul_mx(
                     out=yacc[:, a, :],
-                    lhsT=wd_codes[:, m].bitcast(FP8X4), lhsT_scale=wd_scales[:, m],
+                    lhsT=wd_codes[a // 2][:, a % 2 * P : (a % 2 + 1) * P].bitcast(FP8X4), lhsT_scale=wd_scales[:, m],
                     rhs=h_codes[:, cols].bitcast(FP8X4), rhs_scale=h_scales[:, cols],
                     start=True, stop=True,
                 )
@@ -274,35 +299,35 @@ def tile_list_htabg_gate_none_kernel(
 
         wd_bf = [sb("wd_bf%d" % u, [P, N * PACK // 2], BF16) for u in range(2)]
         lay_wa_scales()
+        lay_wd(0)
+        quant_wd(0)
         last_plane(0)
         last_plane(1)
-        lay_wd(0)
         last_plane(2)
-        quant_x(0)
+        quant_x(0, 256)
         first(0)
         first(1)
         last_plane(3)
         lay_wd(1)
-        quant_x(1)
+        quant_x(256, 512)
         first(2)
         first(3)
         gated(0)
-        quant_wd(0)
         gated(1)
-        quant_x(2)
+        quant_x(512, 768)
         first(4)
         first(5)
         quant_h(0, 256)
         second(0, 256, [0])
         gated(2)
-        quant_x(3)
         gated(3)
-        first(6)
-        first(7)
         quant_wd(1)
         second(0, 256, [1])
         quant_h(256, 512)
         second(256, 512, [0, 1])
+        quant_x(768, 1024)
+        first(6)
+        first(7)
         gated(4)
         gated(5)
         quant_h(512, 640)
@@ -310,8 +335,10 @@ def tile_list_htabg_gate_none_kernel(
         gated(6)
         quant_h(640, 768)
         second_block(5)
-        gated(7)
+        gated(7, 0, 64)
         quant_h(768, 896)
-        quant_h(896, 1024)
+        gated(7, 64, 128)
+        quant_h(896, 960)
+        quant_h(960, 1024)
         second(768, 896, [0, 1], [1])
         second(896, 1024, [0, 1], [1])

@@ -2,7 +2,6 @@ import math
 from contextlib import ExitStack
 
 import concourse.mybir as mybir
-from concourse.masks import make_identity
 
 K, L, R, N, T, J = 512, 512, 512, 512, 2048, 1024
 FLOPS = 2 * J * (K * R + L * R + R * N)
@@ -49,15 +48,15 @@ def tile_list_htabg_gate_none_kernel(
             for r in range(4):
                 queue.dma_start(out=dst[r:P:32, :], in_=src[0, r:16:4, :].bitcast(I32))
 
-        lt = {name: sb(name, shape, dtype) for name, shape, dtype in [("wb_raw", [P, PACK, R], F32)]}
-        late_shapes = [("wa_w_raw", [P, R // 2], I32),
-                       ("tab_w", [P, T], I32),
+        lt = {}
+        late_shapes = [("tab_w", [P, T], I32),
                        ("wa_s_raw", [P, R // 4], I32),
                        ("plane0", [P, T], F32),
                        ("plane1", [P, T], F32),
                        ("plane2", [P, T], F32),
                        ("wd_raw0", [P, PACK, N // 2], F32),
                        ("plane3", [P, T], F32),
+                       ("wa_w_raw", [P, R // 2], I32),
                        ("wd_raw1", [P, PACK, N // 2], F32)]
         late_at = {}
         words = 0
@@ -73,16 +72,21 @@ def tile_list_htabg_gate_none_kernel(
         nc.sync.dma_start(tab_list[:], offs)
         nc.sync.dma_start(head_lists[:], offs2)
         load_scales(nc.sync, tab_s, tab_scales)
-        nc.sync.dma_start(out=lt["wb_raw"][:], in_=wb.rearrange("(p i) r -> p i r", i=PACK))
         nc.scalar.activation(warm[:, 1:2], warm[:, 0:1], SIGMOID)
         ident = sb("ident", [P, P], F32)
-        make_identity(nc, ident[:])
+        zeros = sb("zeros", [P, P], F32, tag="wb_raw")
+        nc.gpsimd.memset(zeros[:], 0.0)
+        nc.gpsimd.affine_select(
+            out=ident[:], in_=zeros[:], compare_op=mybir.AluOpType.not_equal, fill=1.0,
+            base=0, pattern=[[-1, P]], channel_multiplier=1,
+        )
+        lt["wb_raw"] = sb("wb_raw", [P, PACK, R], F32)
+        nc.sync.dma_start(out=lt["wb_raw"][:], in_=wb.rearrange("(p i) r -> p i r", i=PACK))
         turned = ps2.tile([P, P], F32, name="turned", tag="yacc")
         nc.tensor.transpose(turned[:], wgt_rows, ident[:])
         for name, shape, dtype in late_shapes:
             lt[name] = late.tile(shape, dtype, name=name, align_bytes=64, offset=late_at[name])
         nc.gpsimd.memset(lt["wa_s_raw"][:], 0)
-        nc.sync.dma_start(out=lt["wa_w_raw"][:], in_=wa_words[0].bitcast(I32))
         nc.sync.dma_start(out=lt["tab_w"][:], in_=tab_words[0].rearrange("p t i -> p (t i)").bitcast(I32))
         load_scales(nc.sync, lt["wa_s_raw"], wa_scales)
         nc.sync.dma_start(out=lt["plane0"][:], in_=x_planes[0])
@@ -96,6 +100,7 @@ def tile_list_htabg_gate_none_kernel(
 
         load_wd(0)
         nc.sync.dma_start(out=lt["plane3"][:], in_=x_planes[3])
+        nc.sync.dma_start(out=lt["wa_w_raw"][:], in_=wa_words[0].bitcast(I32))
         load_wd(1)
         tab_w, wa_w_raw, wa_s_raw, wb_raw = lt["tab_w"], lt["wa_w_raw"], lt["wa_s_raw"], lt["wb_raw"]
         wd_raw = [lt["wd_raw0"], lt["wd_raw1"]]
@@ -106,10 +111,6 @@ def tile_list_htabg_gate_none_kernel(
 
         wa_codes = sb("wa_codes", [P, 2 * R], U8)
         wa_sc = sb("wa_sc", [P, R], U8)
-        nc.vector.tensor_copy(
-            out=wa_codes[:].bitcast(I32).rearrange("p (t q e) -> p t q e", t=PACK, e=RUN // 2),
-            in_=wa_w_raw[:].rearrange("p (q t e) -> p t q e", t=PACK, e=RUN // 2),
-        )
 
         v_codes = sb("v_codes", [P, J], U32)
         v_scales = sb("v_scales", [P, J], U8)
@@ -212,6 +213,12 @@ def tile_list_htabg_gate_none_kernel(
                 in_=wa_s_raw[:].rearrange("p (q t e) -> p t q e", t=PACK, e=RUN // 4),
             )
 
+        def lay_wa_words():
+            nc.vector.tensor_copy(
+                out=wa_codes[:].bitcast(I32).rearrange("p (t q e) -> p t q e", t=PACK, e=RUN // 2),
+                in_=wa_w_raw[:].rearrange("p (q t e) -> p t q e", t=PACK, e=RUN // 2),
+            )
+
         def last_plane(c):
             gather_chunk(3, c)
             if c < 2:
@@ -302,6 +309,7 @@ def tile_list_htabg_gate_none_kernel(
         lay_wd(0)
         quant_wd(0)
         last_plane(0)
+        lay_wa_words()
         last_plane(1)
         last_plane(2)
         quant_x(0, 256)

@@ -308,6 +308,14 @@ def tile_list_htabg_gate_none_kernel(
         lay_wa_scales()
         lay_wd(0)
         quant_wd(0)
+        for width in (512, 512, NB):
+            idle = ps2.tile([P, width], F32, name="idle", tag="yacc")
+            nc.tensor.matmul_mx(
+                out=idle[:],
+                lhsT=wd_codes[0][:, 0:P].bitcast(FP8X4), lhsT_scale=wd_scales[:, 0:P],
+                rhs=v_codes[:, 0:width].bitcast(FP8X4), rhs_scale=v_scales[:, 0:width],
+                start=True, stop=True,
+            )
         last_plane(0)
         lay_wa_words()
         last_plane(1)

import math
from contextlib import ExitStack

import concourse.mybir as mybir

K, L, R, N, T, J = 512, 512, 512, 512, 2048, 1024
FLOPS = 2 * J * (K * R + L * R + R * N)

F32 = mybir.dt.float32
BF16 = mybir.dt.bfloat16
I32 = mybir.dt.int32
U32 = mybir.dt.uint32
U16 = mybir.dt.uint16
U8 = mybir.dt.uint8
FP8X4 = mybir.dt.float8_e4m3fn_x4
FP4X4 = mybir.dt.float4_e2m1fn_x4
MULT = mybir.AluOpType.mult
SIGMOID = mybir.ActivationFunctionType.Sigmoid

P = 128
PACK = 4
GROUP = 16
NB = 128
CH = 256
RUN = 8


def tile_list_htabg_gate_none_kernel(
    tc, tab_words, tab_scales, xT, wgt2, wa_words, wa_scales, wb, wd, offs, offs2, out
):
    nc = tc.nc
    with ExitStack() as ctx:
        keep = ctx.enter_context(tc.tile_pool(name="keep", bufs=1))
        late = ctx.enter_context(tc.tile_pool(name="late", bufs=1))
        ystage = ctx.enter_context(tc.tile_pool(name="ystage", bufs=10))
        ps1 = ctx.enter_context(tc.psum_pool(name="ps1", bufs=4))
        ps2 = ctx.enter_context(tc.psum_pool(name="ps2", bufs=4))

        def sb(name, shape, dtype, tag=None):
            return keep.tile(shape, dtype, name=name, tag=tag or name, align_bytes=64)

        tab_list = keep.tile([P, J // GROUP], U16, name="tab_list")
        head_lists = keep.tile([P, J // GROUP], U16, name="head_lists")
        tab_s = sb("tab_s", [P, T // 4], I32)
        x_planes = xT.rearrange("(p i) t -> i p t", i=PACK)

        def load_scales(queue, dst, src):
            for r in range(4):
                queue.dma_start(out=dst[r:P:32, :], in_=src[0, r:16:4, :].bitcast(I32))

        lt = {}
        late_shapes = [("tab_w", [P, T], I32),
                       ("wa_s_raw", [P, R // 4], I32),
                       ("plane0", [P, T], F32),
                       ("plane1", [P, T], F32),
                       ("plane2", [P, T], F32),
                       ("wd_raw0", [P, PACK, N // 2], F32),
                       ("plane3", [P, T], F32),
                       ("wa_w_raw", [P, R // 2], I32),
                       ("wd_raw1", [P, PACK, N // 2], F32)]
        late_at = {}
        words = 0
        for name, shape, dtype in late_shapes:
            late_at[name] = 4 * words
            words += math.prod(shape[1:])
        rows_span = late.tile([P, words], F32, name="wgt_rows", align_bytes=64, offset=0)
        wgt_rows = rows_span[:, 0:P]
        warm = sb("warm", [P, 2], F32)
        nc.gpsimd.memset(tab_s[:], 0)
        nc.gpsimd.memset(warm[:, 0:1], 0.0)
        nc.sync.dma_start(out=wgt_rows, in_=wgt2[0:P:8, :].rearrange("a (c x) -> a c x", x=P))
        nc.sync.dma_start(tab_list[:], offs)
        nc.sync.dma_start(head_lists[:], offs2)
        load_scales(nc.sync, tab_s, tab_scales)
        nc.scalar.activation(warm[:, 1:2], warm[:, 0:1], SIGMOID)
        ident = sb("ident", [P, P], F32)
        zeros = sb("zeros", [P, P], F32, tag="wb_raw")
        nc.gpsimd.memset(zeros[:], 0.0)
        nc.gpsimd.affine_select(
            out=ident[:], in_=zeros[:], compare_op=mybir.AluOpType.not_equal, fill=1.0,
            base=0, pattern=[[-1, P]], channel_multiplier=1,
        )
        lt["wb_raw"] = sb("wb_raw", [P, PACK, R], F32)
        nc.sync.dma_start(out=lt["wb_raw"][:], in_=wb.rearrange("(p i) r -> p i r", i=PACK))
        turned = ps2.tile([P, P], F32, name="turned", tag="yacc")
        nc.tensor.transpose(turned[:], wgt_rows, ident[:])
        for name, shape, dtype in late_shapes:
            lt[name] = late.tile(shape, dtype, name=name, align_bytes=64, offset=late_at[name])
        nc.gpsimd.memset(lt["wa_s_raw"][:], 0)
        nc.sync.dma_start(out=lt["tab_w"][:], in_=tab_words[0].rearrange("p t i -> p (t i)").bitcast(I32))
        load_scales(nc.sync, lt["wa_s_raw"], wa_scales)
        nc.sync.dma_start(out=lt["plane0"][:], in_=x_planes[0])
        nc.sync.dma_start(out=lt["plane1"][:], in_=x_planes[1])
        nc.sync.dma_start(out=lt["plane2"][:], in_=x_planes[2])
        wd_rows = wd.rearrange("(q t e) n -> t q e n", t=PACK, e=RUN)

        def load_wd(u):
            for t in range(PACK):
                nc.sync.dma_start(out=lt["wd_raw%d" % u][:, t, :], in_=wd_rows[t][:, :, u * N // 2 : (u + 1) * N // 2])

        load_wd(0)
        nc.sync.dma_start(out=lt["plane3"][:], in_=x_planes[3])
        nc.sync.dma_start(out=lt["wa_w_raw"][:], in_=wa_words[0].bitcast(I32))
        load_wd(1)
        tab_w, wa_w_raw, wa_s_raw, wb_raw = lt["tab_w"], lt["wa_w_raw"], lt["wa_s_raw"], lt["wb_raw"]
        wd_raw = [lt["wd_raw0"], lt["wd_raw1"]]
        planes = [lt["plane%d" % i] for i in range(PACK)]

        spread = sb("spread", [P, 8, 16, 8], F32)
        nc.scalar.copy(out=spread[:], in_=turned[:].rearrange("p (a c) -> p c a", c=8).unsqueeze(3).to_broadcast([P, 8, 16, 8]))

        wa_codes = sb("wa_codes", [P, 2 * R], U8)
        wa_sc = sb("wa_sc", [P, R], U8)

        v_codes = sb("v_codes", [P, J], U32)
        v_scales = sb("v_scales", [P, J], U8)
        nc.vector.tensor_copy(v_scales[:], tab_s[:].bitcast(U8).indirect(tab_list[:]))

        wb_bf = [sb("wb_bf0", [P, R * PACK // 2], BF16), sb("wb_bf1", [P, R * PACK // 2], BF16, tag="tab_s")]
        wb_codes = sb("wb_codes", [P, R], U32)
        wb_scales = sb("wb_scales", [P, R], U8)
        wb_in = wb_raw[:].rearrange("p i (q t d e) -> p t q d i e", t=PACK, d=2, e=4)
        wb_out = wb_bf[0][:].rearrange("p (t q d e i) -> p t q d i e", t=2, d=2, e=4, i=PACK)
        for t in range(2):
            nc.scalar.copy(out=wb_out[:, t], in_=wb_in[:, t])
        nc.vector.tensor_copy(
            out=wb_bf[1][:].rearrange("p (t q e i) -> p t q e i", t=2, e=RUN, i=PACK),
            in_=wb_raw[:].rearrange("p i (q t e) -> p t q e i", t=PACK, e=RUN)[:, 2:4],
        )
        for u in (1, 0):
            cols = slice(u * R // 2, (u + 1) * R // 2)
            nc.vector.quantize_mx(out=wb_codes[:, cols].bitcast(FP8X4), scales=wb_scales[:, cols], in_=wb_bf[u][:])
        wgt = sb("wgt", [P, J], F32, tag="wb_raw")
        for u in range(2):
            back = ps2.tile([P, 4, P], F32, name="back", tag="yacc")
            for c in range(4):
                nc.tensor.transpose(back[:, c, :], spread[:, 4 * u + c].rearrange("p a r -> p (a r)"), ident[:])
            nc.scalar.copy(out=wgt[:, u * 512 : (u + 1) * 512], in_=back[:].rearrange("p c x -> p (c x)"))
        for lo, hi in ((0, 256), (256, 512), (512, 1024)):
            nc.vector.tensor_copy(
                v_codes[:, lo:hi],
                tab_w[:].bitcast(U32).indirect(tab_list[:, lo // GROUP : hi // GROUP]),
            )

        gate = [sb("gate%d" % b, [P, PACK, NB], F32) for b in range(J // NB)]
        for b in range(J // NB):
            cols = slice(b * NB, (b + 1) * NB)
            acc = ps1.tile([P, PACK, NB], F32, name="acc")
            for t in range(PACK):
                m = slice(t * P, (t + 1) * P)
                nc.tensor.matmul_mx(
                    out=acc[:, t, :],
                    lhsT=wb_codes[:, m].bitcast(FP8X4), lhsT_scale=wb_scales[:, m],
                    rhs=v_codes[:, cols].bitcast(FP8X4), rhs_scale=v_scales[:, cols],
                    start=True, stop=True,
                )
            nc.scalar.activation(gate[b][:], acc[:], SIGMOID)

        half = J // 2
        pair01 = sb("pair01", [P, 2, half], F32)
        shared = sb("shared", [P, 5 * CH], F32)
        pair23 = [shared[:, 3 * CH : 5 * CH], sb("pair23", [P, 2 * CH], F32)[:]]
        quad = {2: sb("quad", [P, PACK * CH], F32)[:], 3: shared[:, 0 : PACK * CH]}

        def gather(i, lo, hi, dst):
            nc.vector.tensor_tensor(
                dst,
                planes[i][:].indirect(head_lists[:, lo // GROUP : hi // GROUP]),
                wgt[:, lo:hi],
                MULT,
            )

        def lay_pair(i, lo, hi, src):
            nc.scalar.copy(out=x_bf[:, lo:hi, i : i + 2], in_=src.rearrange("p (i j) -> p j i", i=2))

        def lay_four(c):
            nc.scalar.copy(
                out=x_bf[:, c * CH : (c + 1) * CH, :].rearrange("p (c e) i -> p c i e", e=4),
                in_=quad[c].rearrange("p (i c e) -> p c i e", i=PACK, e=4),
            )

        def gather_chunk(i, c):
            dst = quad[c][:, i * CH : (i + 1) * CH] if c >= 2 else pair23[c][:, (i - 2) * CH : (i - 1) * CH]
            gather(i, c * CH, (c + 1) * CH, dst)

        for i in range(2):
            gather(i, 0, half, pair01[:, i, :])
            gather_chunk(i, 2)
            gather_chunk(i, 3)
        x_bf = sb("x_bf", [P, J, PACK], BF16, tag="wb_codes")
        lay_pair(0, 0, half, pair01[:].rearrange("p i j -> p (i j)"))
        for c in range(4):
            gather_chunk(2, c)

        wd_scales = sb("wd_scales", [P, N], U8)

        x_codes = sb("x_codes", [P, J], U32)
        x_scales = sb("x_scales", [P, J], U8)
        h_bf = sb("h_bf", [P, J, PACK], BF16)
        h_codes = sb("h_codes", [P, J], U32)
        h_scales = sb("h_scales", [P, J], U8)
        out_v = out.rearrange("(a p) j -> p a j", p=P)

        def quant(codes, scales, src, lo, hi):
            nc.vector.quantize_mx(
                out=codes[:, lo:hi].bitcast(FP8X4), scales=scales[:, lo:hi],
                in_=src[:, lo:hi, :].rearrange("p j i -> p (j i)"),
            )

        def lay_wa_scales():
            nc.vector.tensor_copy(
                out=wa_sc[:].bitcast(I32).rearrange("p (t q e) -> p t q e", t=PACK, e=RUN // 4),
                in_=wa_s_raw[:].rearrange("p (q t e) -> p t q e", t=PACK, e=RUN // 4),
            )

        def lay_wa_words():
            nc.vector.tensor_copy(
                out=wa_codes[:].bitcast(I32).rearrange("p (t q e) -> p t q e", t=PACK, e=RUN // 2),
                in_=wa_w_raw[:].rearrange("p (q t e) -> p t q e", t=PACK, e=RUN // 2),
            )

        def last_plane(c):
            gather_chunk(3, c)
            if c < 2:
                lay_pair(2, c * CH, (c + 1) * CH, pair23[c])
            else:
                lay_four(c)

        def quant_x(lo, hi):
            quant(x_codes, x_scales, x_bf, lo, hi)

        ya = [None] * (J // NB)

        def first(b):
            cols = slice(b * NB, (b + 1) * NB)
            acc = ps1.tile([P, PACK, NB], F32, name="acc")
            ya[b] = acc
            for t in range(PACK):
                nc.tensor.matmul_mx(
                    out=acc[:, t, :],
                    lhsT=wa_codes[:, 2 * t * P : 2 * (t + 1) * P].bitcast(FP4X4),
                    lhsT_scale=wa_sc[:, t * P : (t + 1) * P],
                    rhs=x_codes[:, cols].bitcast(FP8X4), rhs_scale=x_scales[:, cols],
                    start=True, stop=True,
                )

        def gated(b, lo=0, hi=NB):
            nc.vector.tensor_tensor(
                h_bf[:, b * NB + lo : b * NB + hi, :].rearrange("p (c e) t -> p c t e", e=4),
                ya[b][:, :, lo:hi].rearrange("p t (c e) -> p c t e", e=4),
                gate[b][:, :, lo:hi].rearrange("p t (c e) -> p c t e", e=4),
                MULT,
            )

        def quant_h(lo, hi):
            quant(h_codes, h_scales, h_bf, lo, hi)

        def lay_wd(u):
            nc.scalar.copy(
                out=wd_bf[u][:].rearrange("p (c e i) -> p c i e", e=4, i=PACK),
                in_=wd_raw[u][:].rearrange("p i (c e) -> p c i e", e=4),
            )

        wd_codes = []

        def quant_wd(u):
            cols = slice(u * N // 2, (u + 1) * N // 2)
            wd_codes.append(sb("wd_codes%d" % u, [P, N // 2], U32, tag=("wd_codes0", "gate2")[u]))
            nc.vector.quantize_mx(out=wd_codes[u][:].bitcast(FP8X4), scales=wd_scales[:, cols], in_=wd_bf[u][:])

        def second(lo, hi, halves, on_vector=()):
            for u in halves:
                if u in on_vector:
                    yacc = ps1.tile([P, 2, hi - lo], F32, name="acc")
                else:
                    yacc = ps2.tile([P, 2, hi - lo], F32, name="yacc")
                for a in range(2):
                    m = slice((2 * u + a) * P, (2 * u + a + 1) * P)
                    nc.tensor.matmul_mx(
                        out=yacc[:, a, :],
                        lhsT=wd_codes[u][:, a * P : (a + 1) * P].bitcast(FP8X4), lhsT_scale=wd_scales[:, m],
                        rhs=h_codes[:, lo:hi].bitcast(FP8X4), rhs_scale=h_scales[:, lo:hi],
                        start=True, stop=True,
                    )
                ysb = ystage.tile([P, 2, hi - lo], F32, name="ysb")
                if u in on_vector:
                    nc.vector.tensor_copy(out=ysb[:], in_=yacc[:])
                else:
                    nc.scalar.copy(out=ysb[:], in_=yacc[:])
                nc.sync.dma_start(out=out_v[:, 2 * u : 2 * u + 2, lo:hi], in_=ysb[:])

        def second_block(b):
            cols = slice(b * NB, (b + 1) * NB)
            yacc = ps2.tile([P, PACK, NB], F32, name="yacc")
            for a in range(PACK):
                m = slice(a * P, (a + 1) * P)
                nc.tensor.matmul_mx(
                    out=yacc[:, a, :],
                    lhsT=wd_codes[a // 2][:, a % 2 * P : (a % 2 + 1) * P].bitcast(FP8X4), lhsT_scale=wd_scales[:, m],
                    rhs=h_codes[:, cols].bitcast(FP8X4), rhs_scale=h_scales[:, cols],
                    start=True, stop=True,
                )
            ysb = ystage.tile([P, PACK, NB], F32, name="ysb")
            nc.scalar.copy(out=ysb[:], in_=yacc[:])
            nc.sync.dma_start(out=out_v[:, :, cols], in_=ysb[:])

        wd_bf = [sb("wd_bf%d" % u, [P, N * PACK // 2], BF16) for u in range(2)]
        lay_wa_scales()
        lay_wd(0)
        quant_wd(0)
        for width in (512, 512, NB):
            idle = ps2.tile([P, width], F32, name="idle", tag="yacc")
            nc.tensor.matmul_mx(
                out=idle[:],
                lhsT=wd_codes[0][:, 0:P].bitcast(FP8X4), lhsT_scale=wd_scales[:, 0:P],
                rhs=v_codes[:, 0:width].bitcast(FP8X4), rhs_scale=v_scales[:, 0:width],
                start=True, stop=True,
            )
        last_plane(0)
        lay_wa_words()
        last_plane(1)
        last_plane(2)
        quant_x(0, 256)
        first(0)
        first(1)
        last_plane(3)
        lay_wd(1)
        quant_x(256, 512)
        first(2)
        first(3)
        gated(0)
        gated(1)
        quant_x(512, 768)
        first(4)
        first(5)
        quant_h(0, 256)
        second(0, 256, [0])
        gated(2)
        gated(3)
        quant_wd(1)
        second(0, 256, [1])
        quant_h(256, 512)
        second(256, 512, [0, 1])
        quant_x(768, 1024)
        first(6)
        first(7)
        gated(4)
        gated(5)
        quant_h(512, 640)
        second_block(4)
        gated(6)
        quant_h(640, 768)
        second_block(5)
        gated(7, 0, 64)
        quant_h(768, 896)
        gated(7, 64, 128)
        quant_h(896, 960)
        quant_h(960, 1024)
        second(768, 896, [0, 1], [1])
        second(896, 1024, [0, 1], [1])
